import numpy as np
import ml_dtypes


def mxq(x, axis, fmt="e4m3"):
    dtype, down = {"e4m3": (ml_dtypes.float8_e4m3fn, 7), "e5m2": (ml_dtypes.float8_e5m2, 14)}[fmt]
    v = np.moveaxis(np.asarray(x, np.float32).astype(ml_dtypes.bfloat16).astype(np.float64), axis, -1)
    blocks = v.reshape(v.shape[:-1] + (-1, 32))
    amax = np.abs(blocks).max(-1, keepdims=True)
    byte = np.maximum(np.where(amax > 0, np.frexp(amax)[1] - 1 + 127, 0) - down, 1)
    scale = np.exp2(byte - 127.0)
    codes = (blocks / scale).astype(np.float32).astype(dtype).astype(np.float64)
    return np.moveaxis((codes * scale).reshape(v.shape), -1, axis)


WIDE = False


def mx_kscale(k):
    if not WIDE:
        return np.ones(k)
    levels = np.array([10, -10, 5, -5, 0])
    if k % 512:
        return np.exp2(np.random.permutation(np.resize(levels, k // 32))).repeat(32)
    a = np.empty((k // 512, 16))
    for p in range(k // 512):
        a[p, :8] = np.random.permutation(np.resize(levels, 8))
        for g in range(8):
            far = levels[np.abs(levels - a[p, g]) >= 10]
            a[p, g + 8] = far[np.random.randint(len(far))]
    return np.exp2(a.ravel()).repeat(32)


BF16 = ml_dtypes.bfloat16


def bf(x):
    return np.asarray(x, np.float32).astype(BF16)


def f64(x):
    return np.asarray(x).astype(np.float64)


E2M1 = np.array([0.0, 0.5, 1.0, 1.5, 2.0, 3.0, 4.0, 6.0, -0.0, -0.5, -1.0, -1.5, -2.0, -3.0, -4.0, -6.0])


def pack_weight(w, fmt):
    k, n = w.shape
    w = f64(bf(w)).reshape(k // 32, 32, n)
    amax = np.abs(w).max(1)
    if fmt == "e4m3":
        byte = np.frexp(amax)[1] - 1 + 127 - 7
    else:
        mant, ex = np.frexp(amax / 6.0)
        byte = np.where(mant > 0.5, ex, ex - 1) + 127
    byte = np.clip(np.where(amax > 0, byte, 1), 1, 254)
    scaled = (w * np.exp2(127.0 - byte)[:, None, :]).reshape(k, n).astype(np.float32)
    by_word = np.ascontiguousarray(scaled.reshape(k // 512, 128, 4, n).transpose(0, 1, 3, 2))
    if fmt == "e4m3":
        words = by_word.astype(ml_dtypes.float8_e4m3fn).view(np.uint8)
    else:
        c = by_word.astype(ml_dtypes.float4_e2m1fn).view(np.uint8) & 0xF
        words = c[..., 0::2] | (c[..., 1::2] << 4)
    return np.ascontiguousarray(words), np.ascontiguousarray(byte.astype(np.uint8).reshape(k // 512, 16, n))


def unpack_weight(words, scales, fmt):
    g, p, n, _ = words.shape
    if fmt == "e4m3":
        vals = np.ascontiguousarray(words).view(ml_dtypes.float8_e4m3fn).astype(np.float64)
    else:
        nib = np.empty((g, p, n, 4), np.uint8)
        nib[..., 0::2] = words & 0xF
        nib[..., 1::2] = words >> 4
        vals = E2M1[nib]
    vals = vals * np.repeat(np.exp2(scales.astype(np.float64) - 127.0), 8, axis=1)[..., None]
    return vals.transpose(0, 1, 3, 2).reshape(g * 512, n)
def pack4(w):
    words, scales = pack_weight(w, "e2m1")
    return words.reshape(words.shape[0], 128, -1), scales


def unpack4(words, scales):
    return unpack_weight(words.reshape(words.shape[0], 128, -1, 2), scales, "e2m1")


def planes(Y):
    n, m = Y.shape
    b = f64(bf(Y)).reshape(n // 32, 32, m)
    amax = np.abs(b).max(1)
    byte = np.clip(np.where(amax > 0, np.frexp(amax)[1] - 1 + 127 - 7, 1), 1, 254)
    codes = (b * np.exp2(127.0 - byte)[:, None, :]).reshape(n, m).astype(np.float32).astype(ml_dtypes.float8_e4m3fn).view(np.uint8)
    words = codes.reshape(n // 512, 128, 4, m).transpose(0, 1, 3, 2)
    return np.ascontiguousarray(words), np.ascontiguousarray(byte.astype(np.uint8).reshape(n // 512, 16, m))


B, P, C, T, N = 1024, 512, 1024, 1024, 1024

def rnd(*shape):
    return np.random.standard_normal(shape)

def setup_inputs():
    a, c, h = mx_kscale(P), mx_kscale(C), mx_kscale(T)
    atoms = 0.7 * rnd(C, T) / np.sqrt(C) / c[:, None]
    atom_words, atom_scales = pack4(atoms)
    return {
        "freq": bf(np.random.uniform(2.0, 40.0, P)),
        "time": bf((np.arange(T) + np.random.uniform(0.0, 1.0, T)) * 2.0 / T - 1.0),
        "phase": bf(np.random.uniform(-np.pi, np.pi, P)),
        "partial_gain": bf(np.exp(0.3 * rnd(P)) * a),
        "amps": bf(rnd(B, P) / np.sqrt(P) / a[None, :]),
        "codes": bf(rnd(B, C) * c[None, :]),
        "atom_words": atom_words,
        "atom_scales": atom_scales,
        "sample_gain": bf(np.random.uniform(0.5, 1.5, T) * h),
        "proj": bf(rnd(T, N) / np.sqrt(T) / h[:, None]),
        "note_gain": bf(np.exp(0.3 * rnd(B))),
        "bias": bf(0.3 * rnd(N)),
        "feature_gain": bf(np.exp(0.8 * rnd(N))),
    }

def reference(freq, time, phase, partial_gain, amps, codes, atom_words, atom_scales, sample_gain, proj, note_gain, bias, feature_gain):
    angle = f64(freq)[:, None] * f64(time)[None, :] + f64(phase)[:, None]
    bank = f64(partial_gain)[:, None] * np.sin(angle)
    tonal = mxq(f64(amps), 1, "e4m3") @ mxq(bank, 0, "e4m3")
    residual = mxq(f64(codes), 1, "e4m3") @ unpack4(atom_words, atom_scales)
    wave = (tonal + residual) * f64(sample_gain)[None, :]
    v = mxq(wave, 1, "e4m3") @ mxq(f64(proj), 0, "e4m3")
    y = np.tanh(v * f64(note_gain)[:, None] + f64(bias)[None, :]) * f64(feature_gain)[None, :]
    Y = y.T
    words, scales = planes(Y)
    return y, words, scales

@@ -1,0 +1,618 @@
+import math
+from contextlib import ExitStack
+
+import concourse.mybir as mybir
+from concourse.masks import make_identity
+
+B, NP, NC, T, N = 1024, 512, 1024, 1024, 1024
+FLOPS = 2 * B * T * (NP + NC) + 2 * B * T * N
+
+F32 = mybir.dt.float32
+BF16 = mybir.dt.bfloat16
+I32 = mybir.dt.int32
+U32 = mybir.dt.uint32
+U8 = mybir.dt.uint8
+FP8X4 = mybir.dt.float8_e4m3fn_x4
+FP4X4 = mybir.dt.float4_e2m1fn_x4
+ALU = mybir.AluOpType
+ACT = mybir.ActivationFunctionType
+
+P = 128
+G = 512
+TILES = B // P
+NUDGE = 1.5e-7
+WORD_STORES = [(0, 2), (2, 4), (4, 6), (6, 7), (7, 8)]
+
+
+def tile_partials_residual_features_k6_kernel(
+    tc, freq, time, phase, partial_gain, amps, codes, atom_words, atom_scales,
+    sample_gain, proj, note_gain, bias, feature_gain, out_0, out_1, out_2,
+):
+    nc = tc.nc
+    with ExitStack() as ctx:
+        keep = ctx.enter_context(tc.tile_pool(name="keep", bufs=1))
+        work = ctx.enter_context(tc.tile_pool(name="work", bufs=2))
+        psum = ctx.enter_context(tc.psum_pool(name="psum", bufs=1))
+        ctx.enter_context(tc.manual_schedule())
+
+        def kept(name, shape, dtype):
+            return keep.tile(shape, dtype, name=name, align_bytes=64)
+
+        def staged(name, shape, dtype, bufs):
+            return work.tile(shape, dtype, name=name, tag=name, bufs=bufs, align_bytes=64)
+
+        def bank_tile(n, shape, dtype):
+            return psum.tile(shape, dtype, name="bank%d" % n, tag="bank%d" % n)
+
+        warm = kept("warm", [P, 1], F32)
+        warm_out = kept("warm_out", [P, 1], F32)
+        ident32 = kept("ident32", [P, P], F32)
+        ident16 = kept("ident16", [P, P], BF16)
+        rows = kept("rows", [P, P], BF16)
+        cols = kept("cols", [P, 16], F32)
+        freq_sb = kept("freq_sb", [P, 4], BF16)
+        phase_sb = kept("phase_sb", [P, 4], BF16)
+        gain_sb = kept("gain_sb", [P, 4], BF16)
+        freq_turns = kept("freq_turns", [P, 4], F32)
+        phase_turns = kept("phase_turns", [P, 4], F32)
+        two_pi = kept("two_pi", [P, 1], F32)
+        time_sb = kept("time_sb", [P, 8], BF16)
+        bias_all = kept("bias_all", [P, N], BF16)
+        fgain_all = kept("fgain_all", [P, N], BF16)
+        atom_raw = kept("atom_raw", [P, 2, 2 * T], U8)
+        atom_codes = kept("atom_codes", [P, 2, 2 * T], U8)
+        atom_sc_raw = kept("atom_sc_raw", [P, 2, T], U8)
+        atom_sc = kept("atom_sc", [P, 2, T], U8)
+        proj_first = [kept("proj_first%d" % g, [P, 4, G], BF16) for g in range(2)]
+        proj_second = kept("proj_second", [P, 4, N], BF16)
+        proj_raw = [proj_first, [proj_second[:, :, :G], proj_second[:, :, G:]]]
+        proj_codes = kept("proj_codes", [P, 2, N], U32)
+        proj_sc = kept("proj_sc", [P, 2, N], U8)
+        bank_codes = kept("bank_codes", [P, T], U32)
+        bank_sc = kept("bank_sc", [P, T], U8)
+        x_codes = kept("x_codes", [P, 3 * TILES * P], U32)
+        x_sc = kept("x_sc", [P, 3 * TILES * P], U8)
+        y_codes = [kept("y_codes%d" % n, [P, 2, P * (b - a)], U32) for n, (a, b) in enumerate(WORD_STORES)]
+        y_sc = kept("y_sc", [P, 2, B], U8)
+        amps_raw = [kept("amps_raw%d" % j, [P, 2, NP], BF16) for j in range(TILES // 2)]
+        codes_raw = [kept("codes_raw%d" % j, [P, 2, NC], BF16) for j in range(TILES // 2)]
+        sines = [kept("sines%d" % h, [P, 4, G], F32) for h in range(2)]
+
+        make_identity(nc, ident16[:])
+        nc.vector.memset(atom_sc_raw[:].bitcast(I32), 0)
+        nc.vector.memset(rows[:], 0.0)
+        make_identity(nc, ident32[:])
+        nc.vector.memset(warm[:], 1.0)
+        nc.scalar.activation(out=warm_out[:], in_=warm[:], func=ACT.Silu)
+
+        def load_x(j):
+            rs = slice(2 * P * j, 2 * P * (j + 1))
+            nc.sync.dma_start(out=amps_raw[j][:], in_=amps[rs, :].rearrange("(i p) k -> p i k", p=P))
+            nc.sync.dma_start(out=codes_raw[j][:], in_=codes[rs, :].rearrange("(i p) k -> p i k", p=P))
+
+        def load_proj(h, dst, fs):
+            by_c = proj[G * h : G * (h + 1), fs].rearrange("(a t c) f -> c a t f", t=4, c=4)
+            for c in range(4):
+                nc.sync.dma_start(out=dst[c:P:4, :, :], in_=by_c[c])
+
+        nc.sync.dma_start(out=time_sb[:], in_=time.rearrange("(p r) -> p r", r=8))
+        nc.sync.dma_start(out=freq_sb[:], in_=freq.rearrange("(p s) -> p s", s=4))
+        nc.sync.dma_start(out=phase_sb[:], in_=phase.rearrange("(p s) -> p s", s=4))
+        load_proj(0, proj_first[0], slice(0, G))
+        load_x(0)
+        nc.sync.dma_start(out=gain_sb[:], in_=partial_gain.rearrange("(p s) -> p s", s=4))
+        nc.sync.dma_start(out=atom_raw[:].bitcast(I32), in_=atom_words.rearrange("g p n -> p g n").bitcast(I32))
+        for q in range(4):
+            nc.sync.dma_start(
+                out=atom_sc_raw[32 * q : 32 * q + 4, :, :].bitcast(I32),
+                in_=atom_scales[:, 4 * q : 4 * q + 4, :].rearrange("g r n -> r g n").bitcast(I32),
+            )
+        for h in range(2):
+            nc.sync.dma_start(
+                out=rows[4 * h : 4 * h + 4, :].rearrange("t (a c) -> t a c", c=4),
+                in_=sample_gain[G * h : G * (h + 1)].rearrange("(a t c) -> t a c", t=4, c=4),
+            )
+        nc.sync.dma_start(out=rows[8:16, :], in_=note_gain.rearrange("(i p) -> i p", p=P))
+        load_x(1)
+        load_proj(1, proj_second, slice(0, N))
+        load_proj(0, proj_first[1], slice(G, N))
+        nc.sync.dma_start(out=bias_all[:], in_=bias.partition_broadcast(P))
+        load_x(2)
+        nc.sync.dma_start(out=fgain_all[:], in_=feature_gain.partition_broadcast(P))
+        load_x(3)
+
+        st = {}
+
+        def x_turn(n, bank):
+            ps = bank_tile(bank, [P, 2, 2, P], F32)
+            for e in range(2):
+                i, q = divmod(2 * n + e, 3)
+                if q == 0:
+                    words = amps_raw[i // 2][:, i % 2, :].bitcast(F32)
+                else:
+                    words = codes_raw[i // 2][:, i % 2, G * (q - 1) : G * q].bitcast(F32)
+                for u in range(2):
+                    nc.tensor.transpose(ps[:, e, u, :], words[:, u:256:2], ident32[:])
+            st["xt", n] = ps
+
+        def x_copy(n, on_vector):
+            grouped = staged("x_grouped", [P, 2 * P * 4], BF16, 5)
+            copy = nc.vector.tensor_copy if on_vector else nc.scalar.copy
+            copy(
+                out=grouped[:].bitcast(F32).rearrange("p (e b u) -> p e b u", e=2, u=2),
+                in_=st["xt", n][:].rearrange("p e u b -> p e b u"),
+            )
+            st["xg", n] = grouped
+
+        def x_quant(n):
+            cs = slice(2 * P * n, 2 * P * (n + 1))
+            nc.vector.quantize_mx(out=x_codes[:, cs].bitcast(FP8X4), scales=x_sc[:, cs], in_=st["xg", n][:])
+
+        def spread_time(bank):
+            st["time"] = bank_tile(bank, [P, 8, P], BF16)
+            for r in range(8):
+                nc.tensor.transpose(st["time"][:, r, :], time_sb[:, r : r + 1].to_broadcast([P, P]), ident16[:])
+
+        def rows_turn(bank):
+            st["rows"] = bank_tile(bank, [P, P], BF16)
+            nc.tensor.transpose(st["rows"][:], rows[:], ident16[:])
+
+        def rows_copy():
+            nc.scalar.copy(out=cols[:], in_=st["rows"][:, :16])
+
+        def scales_out():
+            for q in range(4):
+                eng = nc.sync if q % 2 else nc.scalar
+                eng.dma_start(
+                    out=out_2[:, 4 * q : 4 * q + 4, :].rearrange("g r m -> r g m").bitcast(I32),
+                    in_=y_sc[32 * q : 32 * q + 4, :, :].bitcast(I32),
+                )
+
+        def angle(h, s, on_vector):
+            u = staged("turns", [P, G], F32, 6)
+            dst = u[:].rearrange("p (m r) -> p m r", r=8)
+            src = st["time"][:, :, 64 * h : 64 * (h + 1)].rearrange("p r m -> p m r")
+            f, ph = freq_turns[:, s : s + 1], phase_turns[:, s : s + 1]
+            if on_vector:
+                nc.vector.tensor_scalar(out=dst, in0=src, scalar1=f, scalar2=ph, op0=ALU.mult, op1=ALU.add)
+            else:
+                nc.scalar.activation(out=dst, in_=src, func=ACT.Identity, scale=f, bias=ph)
+            st["u", h, s] = u
+
+        def turns(h, s):
+            k = staged("whole_turns", [P, G], I32, 4)
+            nc.vector.tensor_copy(out=k[:], in_=st["u", h, s][:])
+            st["k", h, s] = k
+
+        def frac(h, s):
+            x = staged("frac", [P, G], F32, 5)
+            nc.vector.tensor_tensor(out=x[:], in0=st["u", h, s][:], in1=st["k", h, s][:], op=ALU.subtract)
+            st["x", h, s] = x
+
+        def sine(h, s):
+            nc.scalar.activation(
+                out=sines[h][:, s, :].rearrange("p (t a c) -> p t a c", t=4, c=4),
+                in_=st["x", h, s][:].rearrange("p (a t c) -> p t a c", t=4, c=4),
+                func=ACT.Sin, scale=two_pi[:],
+            )
+
+        def bank_gain(h):
+            grouped = staged("bank_grouped", [P, G, 4], BF16, 2)
+            nc.vector.tensor_tensor(
+                out=grouped[:].rearrange("p (j e) s -> p j s e", e=2),
+                in0=sines[h][:].rearrange("p s (j e) -> p j s e", e=2),
+                in1=gain_sb[:].unsqueeze(1).unsqueeze(3).to_broadcast([P, G // 2, 4, 2]),
+                op=ALU.mult,
+            )
+            st["bg", h] = grouped
+
+        def bank_quant(h):
+            cs = slice(G * h, G * (h + 1))
+            nc.vector.quantize_mx(
+                out=bank_codes[:, cs].bitcast(FP8X4), scales=bank_sc[:, cs],
+                in_=st["bg", h][:].rearrange("p j s -> p (j s)"),
+            )
+
+        def atom_order(g, h):
+            ws = slice(256 * h, 256 * (h + 1))
+            nc.vector.tensor_copy(
+                out=atom_codes[:, g, :].bitcast(I32)[:, ws].rearrange("p (t a c) -> p t a c", t=4, c=2),
+                in_=atom_raw[:, g, :].bitcast(I32)[:, ws].rearrange("p (a t c) -> p t a c", t=4, c=2),
+            )
+
+        def atom_scale_order(g):
+            nc.vector.tensor_copy(
+                out=atom_sc[:, g, :].bitcast(I32).rearrange("p (h t a) -> p h t a", h=2, t=4),
+                in_=atom_sc_raw[:, g, :].bitcast(I32).rearrange("p (h a t) -> p h t a", h=2, t=4),
+            )
+
+        def proj_group(h, g, on_vector=False):
+            grouped = staged("proj_grouped", [P, G, 4], BF16, 3)
+            copy = nc.vector.tensor_copy if on_vector else nc.scalar.copy
+            copy(
+                out=grouped[:].rearrange("p (c i) t -> p c t i", i=4),
+                in_=proj_raw[h][g][:].rearrange("p t (c i) -> p c t i", i=4),
+            )
+            st["pg", h, g] = grouped
+
+        def proj_quant(h, g):
+            cs = slice(G * g, G * (g + 1))
+            nc.vector.quantize_mx(
+                out=proj_codes[:, h, cs].bitcast(FP8X4), scales=proj_sc[:, h, cs],
+                in_=st["pg", h, g][:].rearrange("p c t -> p (c t)"),
+            )
+
+        def stage1(i, h, bank):
+            ps = bank_tile(bank, [P, 4, P], F32)
+            for t in range(4):
+                c0 = G * h + P * t
+                for g in range(2):
+                    xs = slice(P * (3 * i + 1 + g), P * (3 * i + 2 + g))
+                    nc.tensor.matmul_mx(
+                        out=ps[:, t, :], lhsT=atom_codes[:, g, 2 * c0 : 2 * (c0 + P)].bitcast(FP4X4),
+                        lhsT_scale=atom_sc[:, g, c0 : c0 + P], rhs=x_codes[:, xs].bitcast(FP8X4),
+                        rhs_scale=x_sc[:, xs], start=(g == 0), stop=False,
+                    )
+                xs = slice(P * 3 * i, P * (3 * i + 1))
+                nc.tensor.matmul_mx(
+                    out=ps[:, t, :], lhsT=bank_codes[:, c0 : c0 + P].bitcast(FP8X4),
+                    lhsT_scale=bank_sc[:, c0 : c0 + P], rhs=x_codes[:, xs].bitcast(FP8X4),
+                    rhs_scale=x_sc[:, xs], start=False, stop=True,
+                )
+            st["s1", i, h] = ps
+
+        def wave(i, h):
+            if ("wg", i) not in st:
+                st["wg", i] = staged("wave_grouped", [P, 2, P, 4], BF16, 3)
+            nc.vector.tensor_tensor(
+                out=st["wg", i][:, h, :, :], in0=st["s1", i, h][:].rearrange("p t b -> p b t"),
+                in1=cols[:, 4 * h : 4 * h + 4].unsqueeze(1).to_broadcast([P, P, 4]), op=ALU.mult,
+            )
+
+        def wave_scale(i, h):
+            flat = staged("wave_flat", [P, 4, P], BF16, 3)
+            for t in range(4):
+                nc.scalar.activation(
+                    out=flat[:, t, :], in_=st["s1", i, h][:, t, :], func=ACT.Copy,
+                    scale=cols[:, 4 * h + t : 4 * h + t + 1],
+                )
+            st["wf", i, h] = flat
+
+        def wave_group(i, h):
+            if ("wg", i) not in st:
+                st["wg", i] = staged("wave_grouped", [P, 2, P, 4], BF16, 3)
+            nc.vector.tensor_copy(
+                out=st["wg", i][:, h, :, :].rearrange("p (c i) t -> p c t i", i=4),
+                in_=st["wf", i, h][:].rearrange("p t (c i) -> p c t i", i=4),
+            )
+
+        def wave_quant(i):
+            wc = staged("wave_codes", [P, 2 * P], U32, 6)
+            ws = staged("wave_sc", [P, 2 * P], U8, 6)
+            nc.vector.quantize_mx(
+                out=wc[:].bitcast(FP8X4), scales=ws[:], in_=st["wg", i][:].rearrange("p h b t -> p (h b t)")
+            )
+            st["wq", i] = (wc, ws)
+
+        def stage2(i, g, bank):
+            ps = bank_tile(bank, [P, G], F32)
+            wc, ws = st["wq", i]
+            cs = slice(G * g, G * (g + 1))
+            for h in range(2):
+                nc.tensor.matmul_mx(
+                    out=ps[:], lhsT=wc[:, P * h : P * (h + 1)].bitcast(FP8X4), lhsT_scale=ws[:, P * h : P * (h + 1)],
+                    rhs=proj_codes[:, h, cs].bitcast(FP8X4), rhs_scale=proj_sc[:, h, cs],
+                    start=(h == 0), stop=(h == 1),
+                )
+            st["s2", i, g] = ps
+
+        def affine(i, g):
+            z = staged("pre_tanh", [P, G], F32, 4)
+            nc.vector.scalar_tensor_tensor(
+                out=z[:], in0=st["s2", i, g][:], scalar=cols[:, 8 + i : 9 + i],
+                in1=bias_all[:, G * g : G * (g + 1)], op0=ALU.mult, op1=ALU.add,
+            )
+            st["z", i, g] = z
+
+        def limiter(i, g):
+            th = staged("limited", [P, G], F32, 4)
+            nc.scalar.activation(out=th[:], in_=st["z", i, g][:], func=ACT.Tanh)
+            st["th", i, g] = th
+
+        def gain_out(i, g, on_pool):
+            y = staged("y", [P, G], F32, 5)
+            eng = nc.gpsimd if on_pool else nc.vector
+            eng.tensor_tensor(out=y[:], in0=st["th", i, g][:], in1=fgain_all[:, G * g : G * (g + 1)], op=ALU.mult)
+            st["y", i, g] = y
+            nc.sync.dma_start(out=out_0[P * i : P * (i + 1), G * g : G * (g + 1)], in_=y[:])
+
+        def y_round(i, g, on_vector):
+            yb = staged("y_bf16", [P, G], BF16, 4)
+            copy = nc.vector.tensor_copy if on_vector else nc.scalar.copy
+            copy(
+                out=yb[:].rearrange("p (u m e) -> p u m e", u=2, e=2),
+                in_=st["y", i, g][:].rearrange("p (m u e) -> p u m e", u=2, e=2),
+            )
+            st["yb", i, g] = yb
+
+        def y_turn(i, gs, bank):
+            ps = bank_tile(bank, [P, len(gs), 2, P], F32)
+            for n, g in enumerate(gs):
+                words = st["yb", i, g][:].bitcast(F32)
+                for u in range(2):
+                    nc.tensor.transpose(ps[:, n, u, :], words[:, P * u : P * (u + 1)], ident32[:])
+            st["yt", i, gs] = ps
+
+        def y_copy(i, gs, on_vector):
+            grouped = staged("y_grouped", [P, 2, P * 4], BF16, 3)
+            copy = nc.vector.tensor_copy if on_vector else nc.scalar.copy
+            copy(
+                out=grouped[:, : len(gs), :].bitcast(F32).rearrange("p n (b u) -> p n b u", u=2),
+                in_=st["yt", i, gs][:].rearrange("p n u b -> p n b u"),
+            )
+            for n, g in enumerate(gs):
+                st["yg", i, g] = grouped[:, n, :]
+
+        def y_quant(i, g):
+            cs = slice(P * i, P * (i + 1))
+            n = min(n for n, (a, b) in enumerate(WORD_STORES) if i < b)
+            at = P * (i - WORD_STORES[n][0])
+            nc.vector.quantize_mx(
+                out=y_codes[n][:, g, at : at + P].bitcast(FP8X4), scales=y_sc[:, g, cs], in_=st["yg", i, g]
+            )
+            st["left", n] = st.get(("left", n), 2 * (WORD_STORES[n][1] - WORD_STORES[n][0])) - 1
+            if st["left", n] == 0:
+                ms = slice(P * WORD_STORES[n][0], P * WORD_STORES[n][1])
+                nc.sync.dma_start(out=words_out[:, :, ms], in_=y_codes[n][:].bitcast(I32))
+
+        words_out = out_1.rearrange("g p m t -> p g (m t)").bitcast(I32)
+
+        inv = 1.0 / (2.0 * math.pi)
+        nc.vector.tensor_scalar(out=freq_turns[:], in0=freq_sb[:], scalar1=inv, scalar2=None, op0=ALU.mult)
+        nc.vector.tensor_scalar(out=phase_turns[:], in0=phase_sb[:], scalar1=inv, scalar2=None, op0=ALU.mult)
+        nc.vector.tensor_scalar(out=two_pi[:], in0=warm[:], scalar1=2.0 * math.pi - NUDGE, scalar2=NUDGE, op0=ALU.mult, op1=ALU.add)
+
+        spread_time(0)
+        proj_group(0, 0, True)
+        angle(1, 0, False)
+        angle(1, 2, False)
+        proj_quant(0, 0)
+        angle(0, 0, False)
+        turns(1, 0)
+        x_turn(1, 1)
+        turns(1, 2)
+        angle(1, 3, False)
+        x_turn(0, 2)
+        frac(1, 0)
+        angle(0, 1, False)
+        x_turn(2, 3)
+        turns(0, 0)
+        atom_order(0, 0)
+        angle(0, 2, False)
+        frac(1, 2)
+        angle(1, 1, False)
+        frac(0, 0)
+        angle(0, 3, False)
+        turns(0, 2)
+        atom_scale_order(0)
+        turns(1, 1)
+        sine(0, 0)
+        frac(0, 2)
+        sine(1, 2)
+        rows_turn(4)
+        turns(0, 3)
+        sine(0, 2)
+        frac(1, 1)
+        x_copy(1, False)
+        frac(0, 3)
+        sine(1, 1)
+        atom_order(1, 0)
+        turns(0, 1)
+        x_turn(4, 5)
+        x_quant(1)
+        sine(0, 3)
+        frac(0, 1)
+        x_turn(5, 6)
+        x_copy(4, False)
+        x_turn(3, 7)
+        atom_order(0, 1)
+        atom_order(1, 1)
+        atom_scale_order(1)
+        sine(0, 1)
+        turns(1, 3)
+        x_quant(4)
+        sine(1, 0)
+        frac(1, 3)
+        proj_group(1, 1, False)
+        bank_gain(0)
+        sine(1, 3)
+        bank_quant(0)
+        x_copy(2, False)
+        proj_quant(1, 1)
+        x_turn(6, 0)
+        x_copy(3, False)
+        bank_gain(1)
+        rows_copy()
+        proj_group(1, 0, False)
+        x_turn(7, 1)
+        x_turn(8, 5)
+        x_quant(2)
+        x_turn(10, 3)
+        bank_quant(1)
+        x_copy(6, False)
+        stage1(1, 0, 7)
+        proj_quant(1, 0)
+        x_copy(10, False)
+        x_quant(6)
+        x_copy(8, False)
+        x_quant(3)
+        stage1(1, 1, 4)
+        wave(1, 0)
+        x_copy(7, False)
+        x_quant(8)
+        x_copy(5, False)
+        stage1(2, 0, 0)
+        x_quant(10)
+        wave(1, 1)
+        x_copy(0, False)
+        x_quant(5)
+        stage1(2, 1, 3)
+        proj_group(0, 1, False)
+        x_quant(0)
+        wave_quant(1)
+        x_quant(7)
+        stage1(3, 1, 5)
+        wave(2, 0)
+        wave(2, 1)
+        stage1(0, 0, 7)
+        wave(3, 1)
+        proj_quant(0, 1)
+        stage1(0, 1, 1)
+        wave(0, 0)
+        stage1(4, 1, 6)
+        wave_quant(2)
+        wave(0, 1)
+        stage1(3, 0, 4)
+        wave_quant(0)
+        wave(4, 1)
+        stage2(0, 1, 2)
+        wave(3, 0)
+        stage2(2, 0, 0)
+        affine(0, 1)
+        x_turn(9, 3)
+        affine(2, 0)
+        limiter(0, 1)
+        stage2(1, 0, 5)
+        wave_quant(3)
+        x_copy(9, False)
+        gain_out(0, 1, False)
+        x_turn(11, 7)
+        limiter(2, 0)
+        affine(1, 0)
+        stage2(0, 0, 1)
+        y_round(0, 1, False)
+        gain_out(2, 0, False)
+        stage2(1, 1, 6)
+        x_copy(11, False)
+        x_quant(9)
+        stage2(2, 1, 4)
+        affine(0, 0)
+        y_round(2, 0, False)
+        stage2(3, 0, 2)
+        x_quant(11)
+        limiter(1, 0)
+        affine(2, 1)
+        stage1(4, 0, 0)
+        limiter(0, 0)
+        affine(3, 0)
+        limiter(2, 1)
+        gain_out(0, 0, False)
+        stage1(7, 0, 3)
+        limiter(3, 0)
+        wave(4, 0)
+        y_round(0, 0, False)
+        stage1(7, 1, 5)
+        gain_out(3, 0, False)
+        wave(7, 0)
+        y_round(3, 0, False)
+        y_turn(0, (0, 1), 7)
+        wave_quant(4)
+        stage1(5, 1, 1)
+        wave(7, 1)
+        y_copy(0, (0, 1), False)
+        gain_out(2, 1, False)
+        stage2(4, 0, 4)
+        y_quant(0, 1)
+        y_quant(0, 0)
+        y_round(2, 1, False)
+        wave(5, 1)
+        stage2(4, 1, 2)
+        affine(4, 0)
+        y_turn(2, (0, 1), 0)
+        affine(4, 1)
+        stage1(5, 0, 3)
+        limiter(4, 0)
+        gain_out(1, 0, False)
+        limiter(4, 1)
+        gain_out(4, 0, False)
+        stage1(6, 1, 5)
+        y_round(1, 0, False)
+        wave(5, 0)
+        y_round(4, 0, False)
+        stage2(3, 1, 7)
+        gain_out(4, 1, False)
+        y_copy(2, (0, 1), False)
+        stage1(6, 0, 1)
+        wave(6, 1)
+        y_round(4, 1, False)
+        affine(3, 1)
+        y_turn(4, (0, 1), 4)
+        y_quant(2, 0)
+        wave(6, 0)
+        limiter(3, 1)
+        wave_quant(5)
+        y_copy(4, (0, 1), False)
+        gain_out(3, 1, False)
+        stage2(5, 0, 2)
+        wave_quant(6)
+        y_round(3, 1, False)
+        y_quant(4, 1)
+        stage2(5, 1, 3)
+        y_quant(2, 1)
+        affine(5, 0)
+        stage2(6, 0, 0)
+        affine(5, 1)
+        limiter(5, 0)
+        y_turn(3, (0, 1), 5)
+        affine(6, 0)
+        stage2(6, 1, 7)
+        limiter(5, 1)
+        gain_out(5, 0, False)
+        limiter(6, 0)
+        gain_out(5, 1, False)
+        y_round(5, 0, False)
+        gain_out(6, 0, False)
+        y_round(5, 1, False)
+        affine(6, 1)
+        y_round(6, 0, False)
+        y_turn(5, (0, 1), 1)
+        wave_quant(7)
+        limiter(6, 1)
+        affine(1, 1)
+        stage2(7, 0, 4)
+        y_copy(3, (0, 1), False)
+        y_quant(4, 0)
+        gain_out(6, 1, False)
+        stage2(7, 1, 2)
+        limiter(1, 1)
+        affine(7, 0)
+        y_round(6, 1, False)
+        affine(7, 1)
+        limiter(7, 0)
+        y_turn(6, (0, 1), 3)
+        y_quant(3, 0)
+        y_quant(3, 1)
+        limiter(7, 1)
+        gain_out(1, 1, False)
+        gain_out(7, 0, False)
+        y_copy(6, (0, 1), False)
+        y_round(1, 1, False)
+        gain_out(7, 1, False)
+        y_copy(5, (0, 1), False)
+        y_round(7, 0, True)
+        y_turn(1, (0, 1), 0)
+        y_round(7, 1, True)
+        y_turn(7, (0,), 7)
+        y_quant(6, 1)
+        y_quant(6, 0)
+        y_copy(1, (0, 1), False)
+        y_turn(7, (1,), 6)
+        y_quant(5, 0)
+        y_quant(5, 1)
+        y_copy(7, (1,), False)
+        y_quant(1, 1)
+        y_copy(7, (0,), False)
+        y_quant(1, 0)
+        y_quant(7, 1)
+        y_quant(7, 0)
+        scales_out()

@@ -50,13 +50,14 @@ def tile_partials_residual_features_k6_kernel(
         ident16 = kept("ident16", [P, P], BF16)
         rows = kept("rows", [P, P], BF16)
         cols = kept("cols", [P, 16], F32)
+        cols16 = kept("cols16", [P, 16], BF16)
         freq_sb = kept("freq_sb", [P, 4], BF16)
         phase_sb = kept("phase_sb", [P, 4], BF16)
         gain_sb = kept("gain_sb", [P, 4], BF16)
         freq_turns = kept("freq_turns", [P, 4], F32)
         phase_turns = kept("phase_turns", [P, 4], F32)
         two_pi = kept("two_pi", [P, 1], F32)
-        time_sb = kept("time_sb", [P, 8], BF16)
+        time_sb = kept("time_sb", [P, 2, 4], BF16)
         bias_all = kept("bias_all", [P, N], BF16)
         fgain_all = kept("fgain_all", [P, N], BF16)
         atom_raw = kept("atom_raw", [P, 2, 2 * T], U8)
@@ -95,42 +96,44 @@ def tile_partials_residual_features_k6_kernel(
             for c in range(4):
                 nc.sync.dma_start(out=dst[c:P:4, :, :], in_=by_c[c])
 
-        nc.sync.dma_start(out=time_sb[:], in_=time.rearrange("(p r) -> p r", r=8))
+        nc.sync.dma_start(out=time_sb[:], in_=time.rearrange("(h p r) -> p h r", h=2, r=4))
         nc.sync.dma_start(out=freq_sb[:], in_=freq.rearrange("(p s) -> p s", s=4))
         nc.sync.dma_start(out=phase_sb[:], in_=phase.rearrange("(p s) -> p s", s=4))
         load_proj(0, proj_first[0], slice(0, G))
         load_x(0)
-        nc.sync.dma_start(out=gain_sb[:], in_=partial_gain.rearrange("(p s) -> p s", s=4))
         nc.sync.dma_start(out=atom_raw[:].bitcast(I32), in_=atom_words.rearrange("g p n -> p g n").bitcast(I32))
+        nc.sync.dma_start(out=gain_sb[:], in_=partial_gain.rearrange("(p s) -> p s", s=4))
         for q in range(4):
             nc.sync.dma_start(
                 out=atom_sc_raw[32 * q : 32 * q + 4, :, :].bitcast(I32),
                 in_=atom_scales[:, 4 * q : 4 * q + 4, :].rearrange("g r n -> r g n").bitcast(I32),
             )
+        load_x(1)
         for h in range(2):
             nc.sync.dma_start(
                 out=rows[4 * h : 4 * h + 4, :].rearrange("t (a c) -> t a c", c=4),
                 in_=sample_gain[G * h : G * (h + 1)].rearrange("(a t c) -> t a c", t=4, c=4),
             )
-        nc.sync.dma_start(out=rows[8:16, :], in_=note_gain.rearrange("(i p) -> i p", p=P))
-        load_x(1)
+        for n, vec in enumerate((note_gain, bias, feature_gain)):
+            nc.sync.dma_start(out=rows[8 * n + 8 : 8 * n + 16, :], in_=vec.rearrange("(i p) -> i p", p=P))
         load_proj(1, proj_second, slice(0, N))
-        load_proj(0, proj_first[1], slice(G, N))
-        nc.sync.dma_start(out=bias_all[:], in_=bias.partition_broadcast(P))
         load_x(2)
-        nc.sync.dma_start(out=fgain_all[:], in_=feature_gain.partition_broadcast(P))
+        load_proj(0, proj_first[1], slice(G, N))
         load_x(3)
 
         st = {}
 
+        def x_at(i, q):
+            return 3 * G * (i // 4) + G * q + P * (i % 4)
+
         def x_turn(n, bank):
             ps = bank_tile(bank, [P, 2, 2, P], F32)
+            j, q = divmod(n, 3)
             for e in range(2):
-                i, q = divmod(2 * n + e, 3)
                 if q == 0:
-                    words = amps_raw[i // 2][:, i % 2, :].bitcast(F32)
+                    words = amps_raw[j][:, e, :].bitcast(F32)
                 else:
-                    words = codes_raw[i // 2][:, i % 2, G * (q - 1) : G * q].bitcast(F32)
+                    words = codes_raw[j][:, e, G * (q - 1) : G * q].bitcast(F32)
                 for u in range(2):
                     nc.tensor.transpose(ps[:, e, u, :], words[:, u:256:2], ident32[:])
             st["xt", n] = ps
@@ -145,13 +148,25 @@ def tile_partials_residual_features_k6_kernel(
             st["xg", n] = grouped
 
         def x_quant(n):
-            cs = slice(2 * P * n, 2 * P * (n + 1))
+            j, q = divmod(n, 3)
+            at = x_at(2 * j, q)
+            cs = slice(at, at + 2 * P)
             nc.vector.quantize_mx(out=x_codes[:, cs].bitcast(FP8X4), scales=x_sc[:, cs], in_=st["xg", n][:])
 
-        def spread_time(bank):
-            st["time"] = bank_tile(bank, [P, 8, P], BF16)
+        def spread_time(h, bank):
+            st["time", h] = bank_tile(bank, [P, 4, P], BF16)
+            for r in range(4):
+                nc.tensor.transpose(st["time", h][:, r, :], time_sb[:, h, r : r + 1].to_broadcast([P, P]), ident16[:])
+
+        def spread_row(n, bank):
+            st["row", n] = bank_tile(bank, [P, 8, P], BF16)
             for r in range(8):
-                nc.tensor.transpose(st["time"][:, r, :], time_sb[:, r : r + 1].to_broadcast([P, P]), ident16[:])
+                col = cols16[:, 8 * n + r : 8 * n + r + 1]
+                nc.tensor.transpose(st["row", n][:, r, :], col.to_broadcast([P, P]), ident16[:])
+
+        def row_copy(n, on_vector):
+            copy = nc.vector.tensor_copy if on_vector else nc.scalar.copy
+            copy(out=(bias_all, fgain_all)[n][:], in_=st["row", n][:].rearrange("p r m -> p (r m)"))
 
         def rows_turn(bank):
             st["rows"] = bank_tile(bank, [P, P], BF16)
@@ -159,6 +174,7 @@ def tile_partials_residual_features_k6_kernel(
 
         def rows_copy():
             nc.scalar.copy(out=cols[:], in_=st["rows"][:, :16])
+            nc.scalar.copy(out=cols16[:], in_=st["rows"][:, 16:32])
 
         def scales_out():
             for q in range(4):
@@ -170,8 +186,8 @@ def tile_partials_residual_features_k6_kernel(
 
         def angle(h, s, on_vector):
             u = staged("turns", [P, G], F32, 6)
-            dst = u[:].rearrange("p (m r) -> p m r", r=8)
-            src = st["time"][:, :, 64 * h : 64 * (h + 1)].rearrange("p r m -> p m r")
+            dst = u[:].rearrange("p (m r) -> p m r", r=4)
+            src = st["time", h][:].rearrange("p r m -> p m r")
             f, ph = freq_turns[:, s : s + 1], phase_turns[:, s : s + 1]
             if on_vector:
                 nc.vector.tensor_scalar(out=dst, in0=src, scalar1=f, scalar2=ph, op0=ALU.mult, op1=ALU.add)
@@ -247,13 +263,13 @@ def tile_partials_residual_features_k6_kernel(
             for t in range(4):
                 c0 = G * h + P * t
                 for g in range(2):
-                    xs = slice(P * (3 * i + 1 + g), P * (3 * i + 2 + g))
+                    xs = slice(x_at(i, 1 + g), x_at(i, 1 + g) + P)
                     nc.tensor.matmul_mx(
                         out=ps[:, t, :], lhsT=atom_codes[:, g, 2 * c0 : 2 * (c0 + P)].bitcast(FP4X4),
                         lhsT_scale=atom_sc[:, g, c0 : c0 + P], rhs=x_codes[:, xs].bitcast(FP8X4),
                         rhs_scale=x_sc[:, xs], start=(g == 0), stop=False,
                     )
-                xs = slice(P * 3 * i, P * (3 * i + 1))
+                xs = slice(x_at(i, 0), x_at(i, 0) + P)
                 nc.tensor.matmul_mx(
                     out=ps[:, t, :], lhsT=bank_codes[:, c0 : c0 + P].bitcast(FP8X4),
                     lhsT_scale=bank_sc[:, c0 : c0 + P], rhs=x_codes[:, xs].bitcast(FP8X4),
@@ -269,38 +285,66 @@ def tile_partials_residual_features_k6_kernel(
                 in1=cols[:, 4 * h : 4 * h + 4].unsqueeze(1).to_broadcast([P, P, 4]), op=ALU.mult,
             )
 
-        def wave_scale(i, h):
-            flat = staged("wave_flat", [P, 4, P], BF16, 3)
-            for t in range(4):
-                nc.scalar.activation(
-                    out=flat[:, t, :], in_=st["s1", i, h][:, t, :], func=ACT.Copy,
-                    scale=cols[:, 4 * h + t : 4 * h + t + 1],
+        def wide1(c, h, t, bank):
+            ps = bank_tile(bank, [P, G], F32)
+            c0 = G * h + P * t
+            for g in range(2):
+                xs = slice(x_at(4 * c, 1 + g), x_at(4 * c, 1 + g) + G)
+                nc.tensor.matmul_mx(
+                    out=ps[:], lhsT=atom_codes[:, g, 2 * c0 : 2 * (c0 + P)].bitcast(FP4X4),
+                    lhsT_scale=atom_sc[:, g, c0 : c0 + P], rhs=x_codes[:, xs].bitcast(FP8X4),
+                    rhs_scale=x_sc[:, xs], start=(g == 0), stop=False,
                 )
-            st["wf", i, h] = flat
-
-        def wave_group(i, h):
-            if ("wg", i) not in st:
-                st["wg", i] = staged("wave_grouped", [P, 2, P, 4], BF16, 3)
-            nc.vector.tensor_copy(
-                out=st["wg", i][:, h, :, :].rearrange("p (c i) t -> p c t i", i=4),
-                in_=st["wf", i, h][:].rearrange("p t (c i) -> p c t i", i=4),
+            xs = slice(x_at(4 * c, 0), x_at(4 * c, 0) + G)
+            nc.tensor.matmul_mx(
+                out=ps[:], lhsT=bank_codes[:, c0 : c0 + P].bitcast(FP8X4),
+                lhsT_scale=bank_sc[:, c0 : c0 + P], rhs=x_codes[:, xs].bitcast(FP8X4),
+                rhs_scale=x_sc[:, xs], start=False, stop=True,
             )
+            st["w1", c, h, t] = ps
+
+        def wide_scale(c, h, t, on_vector):
+            if ("wf", c, h) not in st:
+                st["wf", c, h] = staged("wave_flat", [P, 4, G], BF16, 2)
+            dst, src, gain = st["wf", c, h][:, t, :], st["w1", c, h, t][:], cols[:, 4 * h + t : 4 * h + t + 1]
+            if on_vector:
+                nc.vector.tensor_scalar(out=dst, in0=src, scalar1=gain, scalar2=None, op0=ALU.mult)
+            else:
+                nc.scalar.activation(out=dst, in_=src, func=ACT.Copy, scale=gain)
+
+        def wide_group(c, h):
+            grouped = staged("proj_grouped", [P, G, 4], BF16, 3)
+            nc.vector.tensor_copy(
+                out=grouped[:].rearrange("p (c i) t -> p c t i", i=4),
+                in_=st["wf", c, h][:].rearrange("p t (c i) -> p c t i", i=4),
+            )
+            st["wwg", c, h] = grouped
+
+        def wide_quant(c, h):
+            wc = kept("wide_codes%d%d" % (c, h), [P, G], U32)
+            ws = kept("wide_sc%d%d" % (c, h), [P, G], U8)
+            nc.vector.quantize_mx(
+                out=wc[:].bitcast(FP8X4), scales=ws[:], in_=st["wwg", c, h][:].rearrange("p b t -> p (b t)")
+            )
+            for e in range(4):
+                st["wq", 4 * c + e, h] = (wc[:, P * e : P * (e + 1)], ws[:, P * e : P * (e + 1)])
 
         def wave_quant(i):
-            wc = staged("wave_codes", [P, 2 * P], U32, 6)
-            ws = staged("wave_sc", [P, 2 * P], U8, 6)
+            wc = staged("wave_codes", [P, 2 * P], U32, 4)
+            ws = staged("wave_sc", [P, 2 * P], U8, 4)
             nc.vector.quantize_mx(
                 out=wc[:].bitcast(FP8X4), scales=ws[:], in_=st["wg", i][:].rearrange("p h b t -> p (h b t)")
             )
-            st["wq", i] = (wc, ws)
+            for h in range(2):
+                st["wq", i, h] = (wc[:, P * h : P * (h + 1)], ws[:, P * h : P * (h + 1)])
 
         def stage2(i, g, bank):
             ps = bank_tile(bank, [P, G], F32)
-            wc, ws = st["wq", i]
             cs = slice(G * g, G * (g + 1))
             for h in range(2):
+                wc, ws = st["wq", i, h]
                 nc.tensor.matmul_mx(
-                    out=ps[:], lhsT=wc[:, P * h : P * (h + 1)].bitcast(FP8X4), lhsT_scale=ws[:, P * h : P * (h + 1)],
+                    out=ps[:], lhsT=wc.bitcast(FP8X4), lhsT_scale=ws,
                     rhs=proj_codes[:, h, cs].bitcast(FP8X4), rhs_scale=proj_sc[:, h, cs],
                     start=(h == 0), stop=(h == 1),
                 )
@@ -372,247 +416,252 @@ def tile_partials_residual_features_k6_kernel(
         nc.vector.tensor_scalar(out=phase_turns[:], in0=phase_sb[:], scalar1=inv, scalar2=None, op0=ALU.mult)
         nc.vector.tensor_scalar(out=two_pi[:], in0=warm[:], scalar1=2.0 * math.pi - NUDGE, scalar2=NUDGE, op0=ALU.mult, op1=ALU.add)
 
-        spread_time(0)
-        proj_group(0, 0, True)
-        angle(1, 0, False)
-        angle(1, 2, False)
-        proj_quant(0, 0)
-        angle(0, 0, False)
-        turns(1, 0)
-        x_turn(1, 1)
-        turns(1, 2)
-        angle(1, 3, False)
-        x_turn(0, 2)
-        frac(1, 0)
-        angle(0, 1, False)
-        x_turn(2, 3)
-        turns(0, 0)
-        atom_order(0, 0)
+        spread_time(0, 0)
+        angle(0, 3, True)
         angle(0, 2, False)
-        frac(1, 2)
-        angle(1, 1, False)
-        frac(0, 0)
-        angle(0, 3, False)
+        spread_time(1, 1)
+        x_turn(1, 2)
         turns(0, 2)
-        atom_scale_order(0)
-        turns(1, 1)
-        sine(0, 0)
-        frac(0, 2)
-        sine(1, 2)
-        rows_turn(4)
         turns(0, 3)
-        sine(0, 2)
-        frac(1, 1)
-        x_copy(1, False)
-        frac(0, 3)
-        sine(1, 1)
-        atom_order(1, 0)
+        angle(0, 1, False)
+        angle(0, 0, False)
+        angle(1, 0, False)
         turns(0, 1)
-        x_turn(4, 5)
-        x_quant(1)
-        sine(0, 3)
+        frac(0, 3)
+        x_turn(2, 3)
+        angle(1, 1, False)
+        angle(1, 3, False)
         frac(0, 1)
-        x_turn(5, 6)
-        x_copy(4, False)
-        x_turn(3, 7)
-        atom_order(0, 1)
-        atom_order(1, 1)
-        atom_scale_order(1)
         sine(0, 1)
+        turns(1, 0)
+        frac(0, 2)
         turns(1, 3)
-        x_quant(4)
-        sine(1, 0)
+        x_turn(0, 4)
+        angle(1, 2, False)
+        turns(0, 0)
+        frac(1, 0)
+        sine(0, 2)
+        turns(1, 2)
         frac(1, 3)
-        proj_group(1, 1, False)
-        bank_gain(0)
-        sine(1, 3)
-        bank_quant(0)
+        frac(0, 0)
+        x_turn(5, 5)
+        x_turn(4, 6)
         x_copy(2, False)
-        proj_quant(1, 1)
-        x_turn(6, 0)
-        x_copy(3, False)
-        bank_gain(1)
-        rows_copy()
-        proj_group(1, 0, False)
-        x_turn(7, 1)
-        x_turn(8, 5)
-        x_quant(2)
-        x_turn(10, 3)
-        bank_quant(1)
-        x_copy(6, False)
-        stage1(1, 0, 7)
-        proj_quant(1, 0)
-        x_copy(10, False)
-        x_quant(6)
-        x_copy(8, False)
-        x_quant(3)
-        stage1(1, 1, 4)
-        wave(1, 0)
-        x_copy(7, False)
-        x_quant(8)
-        x_copy(5, False)
-        stage1(2, 0, 0)
-        x_quant(10)
-        wave(1, 1)
+        x_copy(1, False)
+        rows_turn(7)
+        x_turn(3, 0)
+        turns(1, 1)
         x_copy(0, False)
-        x_quant(5)
-        stage1(2, 1, 3)
-        proj_group(0, 1, False)
+        sine(0, 0)
+        sine(0, 3)
+        proj_group(0, 0, False)
+        sine(1, 0)
+        atom_order(1, 0)
+        x_quant(2)
+        frac(1, 2)
+        atom_order(1, 1)
+        rows_copy()
+        frac(1, 1)
+        bank_gain(0)
         x_quant(0)
-        wave_quant(1)
-        x_quant(7)
-        stage1(3, 1, 5)
-        wave(2, 0)
-        wave(2, 1)
-        stage1(0, 0, 7)
-        wave(3, 1)
-        proj_quant(0, 1)
-        stage1(0, 1, 1)
+        sine(1, 3)
+        atom_scale_order(1)
+        sine(1, 1)
+        atom_scale_order(0)
+        x_quant(1)
+        spread_row(0, 1)
+        atom_order(0, 0)
+        spread_row(1, 3)
+        sine(1, 2)
+        atom_order(0, 1)
+        bank_quant(0)
+        stage1(1, 0, 2)
+        stage1(0, 0, 4)
+        x_copy(5, False)
+        proj_quant(0, 0)
+        x_turn(7, 7)
+        x_copy(4, False)
+        x_turn(8, 5)
+        proj_group(1, 0, False)
+        bank_gain(1)
+        x_quant(5)
+        wave(1, 0)
+        bank_quant(1)
+        x_copy(8, False)
+        x_turn(6, 6)
+        proj_quant(1, 0)
         wave(0, 0)
-        stage1(4, 1, 6)
-        wave_quant(2)
+        stage1(0, 1, 2)
+        x_quant(4)
+        stage1(1, 1, 5)
+        x_copy(3, False)
+        x_copy(6, False)
+        x_quant(3)
+        x_quant(6)
         wave(0, 1)
-        stage1(3, 0, 4)
+        x_quant(8)
+        x_copy(7, False)
         wave_quant(0)
-        wave(4, 1)
-        stage2(0, 1, 2)
-        wave(3, 0)
-        stage2(2, 0, 0)
-        affine(0, 1)
-        x_turn(9, 3)
-        affine(2, 0)
-        limiter(0, 1)
-        stage2(1, 0, 5)
-        wave_quant(3)
-        x_copy(9, False)
-        gain_out(0, 1, False)
-        x_turn(11, 7)
-        limiter(2, 0)
+        row_copy(0, False)
+        stage1(2, 0, 4)
+        x_quant(7)
+        wave(1, 1)
+        wave(2, 0)
+        row_copy(1, False)
+        wave_quant(1)
+        stage1(2, 1, 0)
+        stage2(0, 0, 6)
+        wave(2, 1)
+        affine(0, 0)
+        stage2(1, 0, 2)
+        stage1(5, 1, 7)
+        proj_group(0, 1, False)
         affine(1, 0)
-        stage2(0, 0, 1)
+        proj_quant(0, 1)
+        wave_quant(2)
+        proj_group(1, 1, False)
+        stage1(4, 1, 1)
+        wave(5, 1)
+        proj_quant(1, 1)
+        limiter(0, 0)
+        stage2(2, 0, 5)
+        wave(4, 1)
+        limiter(1, 0)
+        stage1(4, 0, 4)
+        affine(2, 0)
+        gain_out(1, 0, False)
+        stage2(0, 1, 3)
+        gain_out(0, 0, False)
+        wave(4, 0)
+        affine(0, 1)
+        stage1(5, 0, 0)
+        stage2(2, 1, 6)
+        stage2(1, 1, 2)
+        wave_quant(4)
+        wave(5, 0)
+        affine(2, 1)
+        limiter(0, 1)
+        wave_quant(5)
+        gain_out(0, 1, False)
+        stage1(3, 0, 7)
+        limiter(2, 1)
+        affine(1, 1)
+        y_round(0, 0, False)
+        stage2(4, 0, 1)
+        gain_out(2, 1, False)
+        y_round(1, 0, False)
+        wave(3, 0)
+        stage1(3, 1, 5)
+        limiter(1, 1)
+        limiter(2, 0)
+        y_round(2, 1, False)
+        affine(4, 0)
+        wave(3, 1)
+        stage2(5, 1, 4)
+        stage2(5, 0, 3)
+        limiter(4, 0)
+        affine(5, 1)
         y_round(0, 1, False)
         gain_out(2, 0, False)
-        stage2(1, 1, 6)
-        x_copy(11, False)
-        x_quant(9)
-        stage2(2, 1, 4)
-        affine(0, 0)
-        y_round(2, 0, False)
-        stage2(3, 0, 2)
-        x_quant(11)
-        limiter(1, 0)
-        affine(2, 1)
-        stage1(4, 0, 0)
-        limiter(0, 0)
-        affine(3, 0)
-        limiter(2, 1)
-        gain_out(0, 0, False)
-        stage1(7, 0, 3)
-        limiter(3, 0)
-        wave(4, 0)
-        y_round(0, 0, False)
-        stage1(7, 1, 5)
-        gain_out(3, 0, False)
-        wave(7, 0)
-        y_round(3, 0, False)
-        y_turn(0, (0, 1), 7)
-        wave_quant(4)
-        stage1(5, 1, 1)
-        wave(7, 1)
-        y_copy(0, (0, 1), False)
-        gain_out(2, 1, False)
-        stage2(4, 0, 4)
-        y_quant(0, 1)
-        y_quant(0, 0)
-        y_round(2, 1, False)
-        wave(5, 1)
-        stage2(4, 1, 2)
-        affine(4, 0)
-        y_turn(2, (0, 1), 0)
-        affine(4, 1)
-        stage1(5, 0, 3)
-        limiter(4, 0)
-        gain_out(1, 0, False)
-        limiter(4, 1)
-        gain_out(4, 0, False)
-        stage1(6, 1, 5)
-        y_round(1, 0, False)
-        wave(5, 0)
-        y_round(4, 0, False)
-        stage2(3, 1, 7)
-        gain_out(4, 1, False)
-        y_copy(2, (0, 1), False)
-        stage1(6, 0, 1)
-        wave(6, 1)
-        y_round(4, 1, False)
-        affine(3, 1)
-        y_turn(4, (0, 1), 4)
-        y_quant(2, 0)
-        wave(6, 0)
-        limiter(3, 1)
-        wave_quant(5)
-        y_copy(4, (0, 1), False)
-        gain_out(3, 1, False)
-        stage2(5, 0, 2)
-        wave_quant(6)
-        y_round(3, 1, False)
-        y_quant(4, 1)
-        stage2(5, 1, 3)
-        y_quant(2, 1)
-        affine(5, 0)
-        stage2(6, 0, 0)
-        affine(5, 1)
-        limiter(5, 0)
-        y_turn(3, (0, 1), 5)
-        affine(6, 0)
-        stage2(6, 1, 7)
-        limiter(5, 1)
-        gain_out(5, 0, False)
-        limiter(6, 0)
-        gain_out(5, 1, False)
-        y_round(5, 0, False)
-        gain_out(6, 0, False)
-        y_round(5, 1, False)
-        affine(6, 1)
-        y_round(6, 0, False)
-        y_turn(5, (0, 1), 1)
-        wave_quant(7)
-        limiter(6, 1)
-        affine(1, 1)
-        stage2(7, 0, 4)
-        y_copy(3, (0, 1), False)
-        y_quant(4, 0)
-        gain_out(6, 1, False)
-        stage2(7, 1, 2)
-        limiter(1, 1)
-        affine(7, 0)
-        y_round(6, 1, False)
-        affine(7, 1)
-        limiter(7, 0)
-        y_turn(6, (0, 1), 3)
-        y_quant(3, 0)
-        y_quant(3, 1)
-        limiter(7, 1)
         gain_out(1, 1, False)
-        gain_out(7, 0, False)
-        y_copy(6, (0, 1), False)
+        x_turn(10, 0)
+        wave_quant(3)
+        affine(5, 0)
+        gain_out(4, 0, False)
+        x_turn(11, 6)
+        x_copy(10, False)
+        x_copy(11, False)
+        x_turn(9, 2)
+        x_quant(11)
+        y_turn(0, (0, 1), 7)
+        x_copy(9, False)
+        stage2(4, 1, 1)
+        x_quant(9)
         y_round(1, 1, False)
-        gain_out(7, 1, False)
+        y_round(2, 0, False)
+        x_quant(10)
+        affine(4, 1)
+        limiter(5, 1)
+        limiter(5, 0)
+        stage2(3, 1, 5)
+        stage2(3, 0, 4)
+        y_turn(1, (0, 1), 3)
+        affine(3, 1)
+        affine(3, 0)
+        y_turn(2, (0, 1), 0)
+        gain_out(5, 0, False)
+        gain_out(5, 1, False)
+        stage1(6, 1, 6)
+        limiter(3, 0)
+        y_round(4, 0, False)
+        stage1(6, 0, 2)
+        y_copy(2, (0, 1), False)
+        wave(6, 1)
+        stage1(7, 0, 1)
+        limiter(3, 1)
+        gain_out(3, 0, False)
+        y_round(5, 0, False)
+        stage1(7, 1, 5)
+        wave(6, 0)
+        y_quant(2, 1)
+        y_quant(2, 0)
+        y_round(5, 1, False)
+        wave_quant(6)
+        wave(7, 0)
+        y_copy(0, (0, 1), False)
+        y_turn(5, (0, 1), 4)
+        limiter(4, 1)
+        gain_out(3, 1, False)
+        wave(7, 1)
+        gain_out(4, 1, False)
+        y_round(3, 0, False)
+        stage2(6, 1, 0)
         y_copy(5, (0, 1), False)
-        y_round(7, 0, True)
-        y_turn(1, (0, 1), 0)
+        wave_quant(7)
+        affine(6, 1)
+        y_round(3, 1, False)
+        stage2(6, 0, 6)
+        y_round(4, 1, False)
+        affine(6, 0)
+        limiter(6, 1)
+        y_quant(0, 0)
+        limiter(6, 0)
+        stage2(7, 0, 2)
+        affine(7, 0)
+        gain_out(6, 1, False)
+        stage2(7, 1, 1)
+        y_copy(1, (0, 1), False)
+        affine(7, 1)
+        gain_out(6, 0, False)
+        limiter(7, 0)
+        gain_out(7, 0, False)
+        y_turn(3, (0, 1), 7)
+        y_quant(1, 0)
+        y_quant(0, 1)
+        y_round(6, 0, True)
+        limiter(7, 1)
+        y_turn(4, (0, 1), 5)
+        y_quant(1, 1)
+        y_round(6, 1, False)
+        gain_out(7, 1, False)
+        y_round(7, 0, False)
+        y_copy(3, (0, 1), False)
+        y_copy(4, (0, 1), False)
+        y_quant(5, 1)
+        y_turn(6, (0, 1), 4)
+        y_quant(5, 0)
+        y_turn(7, (0,), 0)
         y_round(7, 1, True)
-        y_turn(7, (0,), 7)
+        y_quant(3, 1)
+        y_quant(3, 0)
+        y_quant(4, 0)
+        y_quant(4, 1)
+        y_turn(7, (1,), 6)
+        y_copy(6, (0, 1), False)
+        y_copy(7, (0,), False)
         y_quant(6, 1)
         y_quant(6, 0)
-        y_copy(1, (0, 1), False)
-        y_turn(7, (1,), 6)
-        y_quant(5, 0)
-        y_quant(5, 1)
         y_copy(7, (1,), False)
-        y_quant(1, 1)
-        y_copy(7, (0,), False)
-        y_quant(1, 0)
-        y_quant(7, 1)
         y_quant(7, 0)
+        y_quant(7, 1)
         scales_out()

@@ -21,6 +21,7 @@ P = 128
 G = 512
 TILES = B // P
 NUDGE = 1.5e-7
+SCALE_STORES = [(0, 6), (6, 8)]
 WORD_STORES = [(0, 2), (2, 4), (4, 6), (6, 7), (7, 8)]
 
 
@@ -59,14 +60,12 @@ def tile_partials_residual_features_k6_kernel(
         two_pi = kept("two_pi", [P, 1], F32)
         time_sb = kept("time_sb", [P, 2, 4], BF16)
         bias_all = kept("bias_all", [P, N], BF16)
-        fgain_all = kept("fgain_all", [P, N], BF16)
+        fgain_all = kept("fgain_all", [P, N], F32)
         atom_raw = kept("atom_raw", [P, 2, 2 * T], U8)
         atom_codes = kept("atom_codes", [P, 2, 2 * T], U8)
         atom_sc_raw = kept("atom_sc_raw", [P, 2, T], U8)
         atom_sc = kept("atom_sc", [P, 2, T], U8)
-        proj_first = [kept("proj_first%d" % g, [P, 4, G], BF16) for g in range(2)]
-        proj_second = kept("proj_second", [P, 4, N], BF16)
-        proj_raw = [proj_first, [proj_second[:, :, :G], proj_second[:, :, G:]]]
+        proj_raw = [kept("proj_raw%d" % h, [P, 4, N], BF16) for h in range(2)]
         proj_codes = kept("proj_codes", [P, 2, N], U32)
         proj_sc = kept("proj_sc", [P, 2, N], U8)
         bank_codes = kept("bank_codes", [P, T], U32)
@@ -74,7 +73,7 @@ def tile_partials_residual_features_k6_kernel(
         x_codes = kept("x_codes", [P, 3 * TILES * P], U32)
         x_sc = kept("x_sc", [P, 3 * TILES * P], U8)
         y_codes = [kept("y_codes%d" % n, [P, 2, P * (b - a)], U32) for n, (a, b) in enumerate(WORD_STORES)]
-        y_sc = kept("y_sc", [P, 2, B], U8)
+        y_sc = [kept("y_sc%d" % n, [P, 2, P * (b - a)], U8) for n, (a, b) in enumerate(SCALE_STORES)]
         amps_raw = [kept("amps_raw%d" % j, [P, 2, NP], BF16) for j in range(TILES // 2)]
         codes_raw = [kept("codes_raw%d" % j, [P, 2, NC], BF16) for j in range(TILES // 2)]
         sines = [kept("sines%d" % h, [P, 4, G], F32) for h in range(2)]
@@ -91,15 +90,14 @@ def tile_partials_residual_features_k6_kernel(
             nc.sync.dma_start(out=amps_raw[j][:], in_=amps[rs, :].rearrange("(i p) k -> p i k", p=P))
             nc.sync.dma_start(out=codes_raw[j][:], in_=codes[rs, :].rearrange("(i p) k -> p i k", p=P))
 
-        def load_proj(h, dst, fs):
-            by_c = proj[G * h : G * (h + 1), fs].rearrange("(a t c) f -> c a t f", t=4, c=4)
+        def load_proj(h):
+            by_c = proj[G * h : G * (h + 1), :].rearrange("(a t c) f -> c a t f", t=4, c=4)
             for c in range(4):
-                nc.sync.dma_start(out=dst[c:P:4, :, :], in_=by_c[c])
+                nc.sync.dma_start(out=proj_raw[h][c:P:4, :, :], in_=by_c[c])
 
         nc.sync.dma_start(out=time_sb[:], in_=time.rearrange("(h p r) -> p h r", h=2, r=4))
         nc.sync.dma_start(out=freq_sb[:], in_=freq.rearrange("(p s) -> p s", s=4))
         nc.sync.dma_start(out=phase_sb[:], in_=phase.rearrange("(p s) -> p s", s=4))
-        load_proj(0, proj_first[0], slice(0, G))
         load_x(0)
         nc.sync.dma_start(out=atom_raw[:].bitcast(I32), in_=atom_words.rearrange("g p n -> p g n").bitcast(I32))
         nc.sync.dma_start(out=gain_sb[:], in_=partial_gain.rearrange("(p s) -> p s", s=4))
@@ -109,6 +107,7 @@ def tile_partials_residual_features_k6_kernel(
                 in_=atom_scales[:, 4 * q : 4 * q + 4, :].rearrange("g r n -> r g n").bitcast(I32),
             )
         load_x(1)
+        load_x(2)
         for h in range(2):
             nc.sync.dma_start(
                 out=rows[4 * h : 4 * h + 4, :].rearrange("t (a c) -> t a c", c=4),
@@ -116,15 +115,14 @@ def tile_partials_residual_features_k6_kernel(
             )
         for n, vec in enumerate((note_gain, bias, feature_gain)):
             nc.sync.dma_start(out=rows[8 * n + 8 : 8 * n + 16, :], in_=vec.rearrange("(i p) -> i p", p=P))
-        load_proj(1, proj_second, slice(0, N))
-        load_x(2)
-        load_proj(0, proj_first[1], slice(G, N))
         load_x(3)
+        load_proj(0)
+        load_proj(1)
 
         st = {}
 
         def x_at(i, q):
-            return 3 * G * (i // 4) + G * q + P * (i % 4)
+            return 6 * P * (i // 2) + 2 * P * q + P * (i % 2)
 
         def x_turn(n, bank):
             ps = bank_tile(bank, [P, 2, 2, P], F32)
@@ -139,19 +137,23 @@ def tile_partials_residual_features_k6_kernel(
             st["xt", n] = ps
 
         def x_copy(n, on_vector):
-            grouped = staged("x_grouped", [P, 2 * P * 4], BF16, 5)
+            j, q = divmod(n, 3)
+            if q == 0:
+                st["xg", j, 0] = staged("amps_grouped", [P, 1, 8 * P], BF16, 2)
+            elif ("xg", j, 1) not in st:
+                st["xg", j, 1] = staged("codes_grouped", [P, 2, 8 * P], BF16, 2)
             copy = nc.vector.tensor_copy if on_vector else nc.scalar.copy
             copy(
-                out=grouped[:].bitcast(F32).rearrange("p (e b u) -> p e b u", e=2, u=2),
+                out=st["xg", j, min(q, 1)][:, max(q - 1, 0), :].bitcast(F32).rearrange("p (e b u) -> p e b u", e=2, u=2),
                 in_=st["xt", n][:].rearrange("p e u b -> p e b u"),
             )
-            st["xg", n] = grouped
 
-        def x_quant(n):
-            j, q = divmod(n, 3)
-            at = x_at(2 * j, q)
-            cs = slice(at, at + 2 * P)
-            nc.vector.quantize_mx(out=x_codes[:, cs].bitcast(FP8X4), scales=x_sc[:, cs], in_=st["xg", n][:])
+        def x_quant(j, part):
+            at = x_at(2 * j, part)
+            cs = slice(at, at + 2 * P * (part + 1))
+            nc.vector.quantize_mx(
+                out=x_codes[:, cs].bitcast(FP8X4), scales=x_sc[:, cs], in_=st["xg", j, part][:].rearrange("p q n -> p (q n)")
+            )
 
         def spread_time(h, bank):
             st["time", h] = bank_tile(bank, [P, 4, P], BF16)
@@ -176,39 +178,30 @@ def tile_partials_residual_features_k6_kernel(
             nc.scalar.copy(out=cols[:], in_=st["rows"][:, :16])
             nc.scalar.copy(out=cols16[:], in_=st["rows"][:, 16:32])
 
-        def scales_out():
-            for q in range(4):
-                eng = nc.sync if q % 2 else nc.scalar
-                eng.dma_start(
-                    out=out_2[:, 4 * q : 4 * q + 4, :].rearrange("g r m -> r g m").bitcast(I32),
-                    in_=y_sc[32 * q : 32 * q + 4, :, :].bitcast(I32),
-                )
-
         def angle(h, s, on_vector):
-            u = staged("turns", [P, G], F32, 6)
-            dst = u[:].rearrange("p (m r) -> p m r", r=4)
-            src = st["time", h][:].rearrange("p r m -> p m r")
+            if ("u", h, s // 2) not in st:
+                st["u", h, s // 2] = staged("turns", [P, 2, G], F32, 3)
+            dst = st["u", h, s // 2][:, s % 2, :].rearrange("p (t a c) -> p t a c", t=4, c=4)
+            src = st["time", h][:].rearrange("p c (a t) -> p t a c", t=4)
             f, ph = freq_turns[:, s : s + 1], phase_turns[:, s : s + 1]
             if on_vector:
                 nc.vector.tensor_scalar(out=dst, in0=src, scalar1=f, scalar2=ph, op0=ALU.mult, op1=ALU.add)
             else:
                 nc.scalar.activation(out=dst, in_=src, func=ACT.Identity, scale=f, bias=ph)
-            st["u", h, s] = u
 
         def turns(h, s):
-            k = staged("whole_turns", [P, G], I32, 4)
+            k = staged("whole_turns", [P, 2, G], I32, 2)
             nc.vector.tensor_copy(out=k[:], in_=st["u", h, s][:])
             st["k", h, s] = k
 
         def frac(h, s):
-            x = staged("frac", [P, G], F32, 5)
+            x = staged("frac", [P, 2, G], F32, 3)
             nc.vector.tensor_tensor(out=x[:], in0=st["u", h, s][:], in1=st["k", h, s][:], op=ALU.subtract)
             st["x", h, s] = x
 
         def sine(h, s):
             nc.scalar.activation(
-                out=sines[h][:, s, :].rearrange("p (t a c) -> p t a c", t=4, c=4),
-                in_=st["x", h, s][:].rearrange("p (a t c) -> p t a c", t=4, c=4),
+                out=sines[h][:, 2 * s : 2 * s + 2, :], in_=st["x", h, s][:],
                 func=ACT.Sin, scale=two_pi[:],
             )
 
@@ -229,17 +222,17 @@ def tile_partials_residual_features_k6_kernel(
                 in_=st["bg", h][:].rearrange("p j s -> p (j s)"),
             )
 
-        def atom_order(g, h):
+        def atom_order(h):
             ws = slice(256 * h, 256 * (h + 1))
             nc.vector.tensor_copy(
-                out=atom_codes[:, g, :].bitcast(I32)[:, ws].rearrange("p (t a c) -> p t a c", t=4, c=2),
-                in_=atom_raw[:, g, :].bitcast(I32)[:, ws].rearrange("p (a t c) -> p t a c", t=4, c=2),
+                out=atom_codes[:].bitcast(I32)[:, :, ws].rearrange("p g (t a c) -> p g t a c", t=4, c=2),
+                in_=atom_raw[:].bitcast(I32)[:, :, ws].rearrange("p g (a t c) -> p g t a c", t=4, c=2),
             )
 
-        def atom_scale_order(g):
+        def atom_scale_order():
             nc.vector.tensor_copy(
-                out=atom_sc[:, g, :].bitcast(I32).rearrange("p (h t a) -> p h t a", h=2, t=4),
-                in_=atom_sc_raw[:, g, :].bitcast(I32).rearrange("p (h a t) -> p h t a", h=2, t=4),
+                out=atom_sc[:].bitcast(I32).rearrange("p g (h t a) -> p (g h) t a", h=2, t=4),
+                in_=atom_sc_raw[:].bitcast(I32).rearrange("p g (h a t) -> p (g h) t a", h=2, t=4),
             )
 
         def proj_group(h, g, on_vector=False):
@@ -247,7 +240,7 @@ def tile_partials_residual_features_k6_kernel(
             copy = nc.vector.tensor_copy if on_vector else nc.scalar.copy
             copy(
                 out=grouped[:].rearrange("p (c i) t -> p c t i", i=4),
-                in_=proj_raw[h][g][:].rearrange("p t (c i) -> p c t i", i=4),
+                in_=proj_raw[h][:, :, G * g : G * (g + 1)].rearrange("p t (c i) -> p c t i", i=4),
             )
             st["pg", h, g] = grouped
 
@@ -284,50 +277,6 @@ def tile_partials_residual_features_k6_kernel(
                 out=st["wg", i][:, h, :, :], in0=st["s1", i, h][:].rearrange("p t b -> p b t"),
                 in1=cols[:, 4 * h : 4 * h + 4].unsqueeze(1).to_broadcast([P, P, 4]), op=ALU.mult,
             )
-
-        def wide1(c, h, t, bank):
-            ps = bank_tile(bank, [P, G], F32)
-            c0 = G * h + P * t
-            for g in range(2):
-                xs = slice(x_at(4 * c, 1 + g), x_at(4 * c, 1 + g) + G)
-                nc.tensor.matmul_mx(
-                    out=ps[:], lhsT=atom_codes[:, g, 2 * c0 : 2 * (c0 + P)].bitcast(FP4X4),
-                    lhsT_scale=atom_sc[:, g, c0 : c0 + P], rhs=x_codes[:, xs].bitcast(FP8X4),
-                    rhs_scale=x_sc[:, xs], start=(g == 0), stop=False,
-                )
-            xs = slice(x_at(4 * c, 0), x_at(4 * c, 0) + G)
-            nc.tensor.matmul_mx(
-                out=ps[:], lhsT=bank_codes[:, c0 : c0 + P].bitcast(FP8X4),
-                lhsT_scale=bank_sc[:, c0 : c0 + P], rhs=x_codes[:, xs].bitcast(FP8X4),
-                rhs_scale=x_sc[:, xs], start=False, stop=True,
-            )
-            st["w1", c, h, t] = ps
-
-        def wide_scale(c, h, t, on_vector):
-            if ("wf", c, h) not in st:
-                st["wf", c, h] = staged("wave_flat", [P, 4, G], BF16, 2)
-            dst, src, gain = st["wf", c, h][:, t, :], st["w1", c, h, t][:], cols[:, 4 * h + t : 4 * h + t + 1]
-            if on_vector:
-                nc.vector.tensor_scalar(out=dst, in0=src, scalar1=gain, scalar2=None, op0=ALU.mult)
-            else:
-                nc.scalar.activation(out=dst, in_=src, func=ACT.Copy, scale=gain)
-
-        def wide_group(c, h):
-            grouped = staged("proj_grouped", [P, G, 4], BF16, 3)
-            nc.vector.tensor_copy(
-                out=grouped[:].rearrange("p (c i) t -> p c t i", i=4),
-                in_=st["wf", c, h][:].rearrange("p t (c i) -> p c t i", i=4),
-            )
-            st["wwg", c, h] = grouped
-
-        def wide_quant(c, h):
-            wc = kept("wide_codes%d%d" % (c, h), [P, G], U32)
-            ws = kept("wide_sc%d%d" % (c, h), [P, G], U8)
-            nc.vector.quantize_mx(
-                out=wc[:].bitcast(FP8X4), scales=ws[:], in_=st["wwg", c, h][:].rearrange("p b t -> p (b t)")
-            )
-            for e in range(4):
-                st["wq", 4 * c + e, h] = (wc[:, P * e : P * (e + 1)], ws[:, P * e : P * (e + 1)])
 
         def wave_quant(i):
             wc = staged("wave_codes", [P, 2 * P], U32, 4)
@@ -398,16 +347,25 @@ def tile_partials_residual_features_k6_kernel(
                 st["yg", i, g] = grouped[:, n, :]
 
         def y_quant(i, g):
-            cs = slice(P * i, P * (i + 1))
             n = min(n for n, (a, b) in enumerate(WORD_STORES) if i < b)
-            at = P * (i - WORD_STORES[n][0])
+            m = min(m for m, (a, b) in enumerate(SCALE_STORES) if i < b)
+            at, sat = P * (i - WORD_STORES[n][0]), P * (i - SCALE_STORES[m][0])
             nc.vector.quantize_mx(
-                out=y_codes[n][:, g, at : at + P].bitcast(FP8X4), scales=y_sc[:, g, cs], in_=st["yg", i, g]
+                out=y_codes[n][:, g, at : at + P].bitcast(FP8X4), scales=y_sc[m][:, g, sat : sat + P], in_=st["yg", i, g]
             )
             st["left", n] = st.get(("left", n), 2 * (WORD_STORES[n][1] - WORD_STORES[n][0])) - 1
             if st["left", n] == 0:
                 ms = slice(P * WORD_STORES[n][0], P * WORD_STORES[n][1])
                 nc.sync.dma_start(out=words_out[:, :, ms], in_=y_codes[n][:].bitcast(I32))
+            st["sleft", m] = st.get(("sleft", m), 2 * (SCALE_STORES[m][1] - SCALE_STORES[m][0])) - 1
+            if st["sleft", m] == 0:
+                ms = slice(P * SCALE_STORES[m][0], P * SCALE_STORES[m][1])
+                for q in range(4):
+                    eng = nc.scalar if m == 1 and q % 2 == 0 else nc.sync
+                    eng.dma_start(
+                        out=out_2[:, 4 * q : 4 * q + 4, ms].rearrange("g r m -> r g m").bitcast(I32),
+                        in_=y_sc[m][32 * q : 32 * q + 4, :, :].bitcast(I32),
+                    )
 
         words_out = out_1.rearrange("g p m t -> p g (m t)").bitcast(I32)
 
@@ -417,251 +375,231 @@ def tile_partials_residual_features_k6_kernel(
         nc.vector.tensor_scalar(out=two_pi[:], in0=warm[:], scalar1=2.0 * math.pi - NUDGE, scalar2=NUDGE, op0=ALU.mult, op1=ALU.add)
 
         spread_time(0, 0)
-        angle(0, 3, True)
-        angle(0, 2, False)
+        angle(0, 1, True)
         spread_time(1, 1)
-        x_turn(1, 2)
-        turns(0, 2)
-        turns(0, 3)
-        angle(0, 1, False)
         angle(0, 0, False)
-        angle(1, 0, False)
-        turns(0, 1)
-        frac(0, 3)
-        x_turn(2, 3)
-        angle(1, 1, False)
-        angle(1, 3, False)
-        frac(0, 1)
-        sine(0, 1)
-        turns(1, 0)
-        frac(0, 2)
-        turns(1, 3)
-        x_turn(0, 4)
-        angle(1, 2, False)
         turns(0, 0)
-        frac(1, 0)
-        sine(0, 2)
-        turns(1, 2)
-        frac(1, 3)
         frac(0, 0)
-        x_turn(5, 5)
-        x_turn(4, 6)
+        x_turn(2, 2)
+        x_turn(0, 3)
+        x_turn(1, 4)
+        angle(0, 3, False)
+        angle(0, 2, False)
+        angle(1, 0, False)
+        angle(1, 1, False)
         x_copy(2, False)
+        angle(1, 3, False)
         x_copy(1, False)
-        rows_turn(7)
-        x_turn(3, 0)
+        angle(1, 2, False)
+        sine(0, 0)
+        x_turn(3, 5)
+        x_turn(4, 6)
+        x_turn(5, 7)
+        x_turn(8, 0)
+        x_turn(6, 2)
+        rows_turn(4)
+        x_turn(7, 1)
+        atom_order(0)
+        turns(0, 1)
+        turns(1, 0)
+        frac(0, 1)
+        frac(1, 0)
+        atom_order(1)
         turns(1, 1)
         x_copy(0, False)
-        sine(0, 0)
-        sine(0, 3)
-        proj_group(0, 0, False)
-        sine(1, 0)
-        atom_order(1, 0)
-        x_quant(2)
-        frac(1, 2)
-        atom_order(1, 1)
-        rows_copy()
+        x_quant(0, 0)
+        x_quant(0, 1)
         frac(1, 1)
-        bank_gain(0)
-        x_quant(0)
-        sine(1, 3)
-        atom_scale_order(1)
-        sine(1, 1)
-        atom_scale_order(0)
-        x_quant(1)
-        spread_row(0, 1)
-        atom_order(0, 0)
-        spread_row(1, 3)
-        sine(1, 2)
-        atom_order(0, 1)
-        bank_quant(0)
-        stage1(1, 0, 2)
-        stage1(0, 0, 4)
-        x_copy(5, False)
-        proj_quant(0, 0)
-        x_turn(7, 7)
+        sine(0, 1)
+        sine(1, 0)
         x_copy(4, False)
-        x_turn(8, 5)
-        proj_group(1, 0, False)
-        bank_gain(1)
-        x_quant(5)
-        wave(1, 0)
-        bank_quant(1)
-        x_copy(8, False)
-        x_turn(6, 6)
-        proj_quant(1, 0)
-        wave(0, 0)
-        stage1(0, 1, 2)
-        x_quant(4)
-        stage1(1, 1, 5)
         x_copy(3, False)
+        x_copy(5, False)
         x_copy(6, False)
-        x_quant(3)
-        x_quant(6)
-        wave(0, 1)
-        x_quant(8)
+        bank_gain(0)
+        x_quant(1, 1)
+        x_quant(1, 0)
+        bank_quant(0)
+        atom_scale_order()
+        rows_copy()
+        spread_row(1, 3)
+        spread_row(0, 6)
+        x_turn(9, 5)
+        x_turn(11, 7)
+        x_turn(10, 2)
+        sine(1, 1)
         x_copy(7, False)
-        wave_quant(0)
+        x_copy(8, False)
         row_copy(0, False)
-        stage1(2, 0, 4)
-        x_quant(7)
-        wave(1, 1)
-        wave(2, 0)
-        row_copy(1, False)
-        wave_quant(1)
-        stage1(2, 1, 0)
-        stage2(0, 0, 6)
-        wave(2, 1)
-        affine(0, 0)
-        stage2(1, 0, 2)
-        stage1(5, 1, 7)
-        proj_group(0, 1, False)
-        affine(1, 0)
-        proj_quant(0, 1)
-        wave_quant(2)
-        proj_group(1, 1, False)
-        stage1(4, 1, 1)
-        wave(5, 1)
-        proj_quant(1, 1)
-        limiter(0, 0)
-        stage2(2, 0, 5)
-        wave(4, 1)
-        limiter(1, 0)
-        stage1(4, 0, 4)
-        affine(2, 0)
-        gain_out(1, 0, False)
-        stage2(0, 1, 3)
-        gain_out(0, 0, False)
-        wave(4, 0)
-        affine(0, 1)
-        stage1(5, 0, 0)
-        stage2(2, 1, 6)
-        stage2(1, 1, 2)
-        wave_quant(4)
-        wave(5, 0)
-        affine(2, 1)
-        limiter(0, 1)
-        wave_quant(5)
-        gain_out(0, 1, False)
-        stage1(3, 0, 7)
-        limiter(2, 1)
-        affine(1, 1)
-        y_round(0, 0, False)
-        stage2(4, 0, 1)
-        gain_out(2, 1, False)
-        y_round(1, 0, False)
-        wave(3, 0)
-        stage1(3, 1, 5)
-        limiter(1, 1)
-        limiter(2, 0)
-        y_round(2, 1, False)
-        affine(4, 0)
-        wave(3, 1)
-        stage2(5, 1, 4)
-        stage2(5, 0, 3)
-        limiter(4, 0)
-        affine(5, 1)
-        y_round(0, 1, False)
-        gain_out(2, 0, False)
-        gain_out(1, 1, False)
-        x_turn(10, 0)
-        wave_quant(3)
-        affine(5, 0)
-        gain_out(4, 0, False)
-        x_turn(11, 6)
-        x_copy(10, False)
-        x_copy(11, False)
-        x_turn(9, 2)
-        x_quant(11)
-        y_turn(0, (0, 1), 7)
         x_copy(9, False)
-        stage2(4, 1, 1)
-        x_quant(9)
-        y_round(1, 1, False)
-        y_round(2, 0, False)
-        x_quant(10)
-        affine(4, 1)
-        limiter(5, 1)
-        limiter(5, 0)
-        stage2(3, 1, 5)
-        stage2(3, 0, 4)
-        y_turn(1, (0, 1), 3)
+        x_copy(11, False)
+        x_copy(10, False)
+        proj_group(0, 1, False)
+        proj_group(1, 1, False)
+        bank_gain(1)
+        x_quant(3, 0)
+        stage1(2, 0, 4)
+        stage1(0, 0, 1)
+        bank_quant(1)
+        wave(2, 0)
+        x_quant(2, 1)
+        x_quant(3, 1)
+        stage1(0, 1, 0)
+        wave(0, 1)
+        wave(0, 0)
+        x_quant(2, 0)
+        stage1(2, 1, 6)
+        stage1(1, 0, 5)
+        stage1(1, 1, 7)
+        proj_quant(0, 1)
+        stage1(3, 1, 2)
+        wave(2, 1)
+        wave(1, 0)
+        wave_quant(2)
+        wave_quant(0)
+        proj_quant(1, 1)
+        proj_group(0, 0, False)
+        proj_group(1, 0, False)
+        wave(3, 1)
+        wave(1, 1)
+        stage1(3, 0, 4)
+        stage2(0, 1, 0)
+        wave(3, 0)
+        affine(0, 1)
+        wave_quant(3)
+        wave_quant(1)
+        proj_quant(0, 0)
+        stage2(2, 1, 1)
+        stage1(5, 1, 6)
+        stage1(4, 1, 5)
+        stage2(3, 1, 2)
+        proj_quant(1, 0)
+        affine(2, 1)
+        row_copy(1, False)
+        limiter(0, 1)
+        stage2(1, 0, 7)
+        stage2(0, 0, 4)
+        stage1(5, 0, 0)
+        stage2(3, 0, 1)
+        stage1(4, 0, 3)
+        gain_out(0, 1, True)
+        limiter(2, 1)
         affine(3, 1)
+        wave(4, 1)
+        affine(1, 0)
+        affine(0, 0)
+        wave(5, 1)
+        wave(5, 0)
         affine(3, 0)
-        y_turn(2, (0, 1), 0)
-        gain_out(5, 0, False)
-        gain_out(5, 1, False)
-        stage1(6, 1, 6)
-        limiter(3, 0)
-        y_round(4, 0, False)
-        stage1(6, 0, 2)
-        y_copy(2, (0, 1), False)
-        wave(6, 1)
-        stage1(7, 0, 1)
+        wave(4, 0)
+        gain_out(2, 1, True)
         limiter(3, 1)
-        gain_out(3, 0, False)
-        y_round(5, 0, False)
+        y_round(0, 1, False)
+        y_round(2, 1, False)
+        limiter(0, 0)
+        limiter(3, 0)
+        limiter(1, 0)
+        gain_out(3, 1, True)
+        wave_quant(5)
+        gain_out(0, 0, False)
+        wave_quant(4)
+        y_round(0, 0, False)
+        y_round(3, 1, False)
+        gain_out(1, 0, True)
+        stage2(1, 1, 2)
         stage1(7, 1, 5)
-        wave(6, 0)
-        y_quant(2, 1)
-        y_quant(2, 0)
-        y_round(5, 1, False)
-        wave_quant(6)
-        wave(7, 0)
+        stage2(5, 1, 7)
+        stage2(2, 0, 4)
+        affine(1, 1)
+        limiter(1, 1)
+        gain_out(1, 1, True)
+        stage2(4, 0, 6)
+        y_turn(0, (0, 1), 0)
+        stage2(4, 1, 1)
+        stage2(5, 0, 3)
+        stage1(7, 0, 2)
+        affine(5, 1)
+        affine(2, 0)
+        gain_out(3, 0, False)
+        y_round(1, 0, False)
+        limiter(5, 1)
         y_copy(0, (0, 1), False)
-        y_turn(5, (0, 1), 4)
-        limiter(4, 1)
-        gain_out(3, 1, False)
+        limiter(2, 0)
+        gain_out(5, 1, True)
         wave(7, 1)
+        affine(4, 0)
+        affine(4, 1)
+        affine(5, 0)
+        wave(7, 0)
+        y_round(1, 1, False)
+        stage1(6, 0, 7)
+        y_turn(1, (0, 1), 4)
+        stage1(6, 1, 0)
+        limiter(4, 1)
+        limiter(5, 0)
+        gain_out(2, 0, False)
+        y_quant(0, 0)
+        wave_quant(7)
         gain_out(4, 1, False)
         y_round(3, 0, False)
-        stage2(6, 1, 0)
-        y_copy(5, (0, 1), False)
-        wave_quant(7)
-        affine(6, 1)
-        y_round(3, 1, False)
-        stage2(6, 0, 6)
-        y_round(4, 1, False)
-        affine(6, 0)
-        limiter(6, 1)
-        y_quant(0, 0)
-        limiter(6, 0)
-        stage2(7, 0, 2)
-        affine(7, 0)
-        gain_out(6, 1, False)
-        stage2(7, 1, 1)
+        y_round(2, 0, False)
+        limiter(4, 0)
         y_copy(1, (0, 1), False)
-        affine(7, 1)
-        gain_out(6, 0, False)
-        limiter(7, 0)
-        gain_out(7, 0, False)
-        y_turn(3, (0, 1), 7)
-        y_quant(1, 0)
-        y_quant(0, 1)
-        y_round(6, 0, True)
-        limiter(7, 1)
-        y_turn(4, (0, 1), 5)
+        stage2(7, 0, 5)
+        y_turn(2, (0, 1), 6)
+        y_turn(3, (0, 1), 1)
+        stage2(7, 1, 3)
+        wave(6, 0)
+        wave(6, 1)
+        gain_out(5, 0, True)
+        affine(7, 0)
+        wave_quant(6)
+        y_round(5, 1, True)
         y_quant(1, 1)
-        y_round(6, 1, False)
-        gain_out(7, 1, False)
-        y_round(7, 0, False)
+        y_quant(0, 1)
+        gain_out(4, 0, False)
+        y_quant(1, 0)
+        stage2(6, 1, 2)
+        stage2(6, 0, 4)
+        affine(6, 1)
+        affine(6, 0)
+        affine(7, 1)
+        y_round(4, 1, False)
+        y_copy(2, (0, 1), False)
+        limiter(7, 0)
+        y_round(5, 0, False)
+        y_round(4, 0, False)
         y_copy(3, (0, 1), False)
-        y_copy(4, (0, 1), False)
-        y_quant(5, 1)
-        y_turn(6, (0, 1), 4)
-        y_quant(5, 0)
-        y_turn(7, (0,), 0)
-        y_round(7, 1, True)
-        y_quant(3, 1)
+        limiter(6, 1)
         y_quant(3, 0)
-        y_quant(4, 0)
+        y_quant(2, 1)
+        y_quant(2, 0)
+        y_quant(3, 1)
+        limiter(6, 0)
+        gain_out(6, 1, False)
+        y_turn(4, (0, 1), 7)
+        y_turn(5, (0, 1), 0)
+        y_copy(4, (0, 1), False)
+        y_copy(5, (0, 1), False)
+        limiter(7, 1)
+        gain_out(6, 0, False)
         y_quant(4, 1)
-        y_turn(7, (1,), 6)
+        y_quant(4, 0)
+        y_quant(5, 1)
+        y_quant(5, 0)
+        y_round(6, 1, True)
+        y_round(6, 0, False)
+        gain_out(7, 0, True)
+        gain_out(7, 1, False)
+        y_round(7, 1, True)
+        y_round(7, 0, False)
+        y_turn(6, (0, 1), 5)
         y_copy(6, (0, 1), False)
+        y_turn(7, (0,), 2)
+        y_turn(7, (1,), 4)
         y_copy(7, (0,), False)
-        y_quant(6, 1)
         y_quant(6, 0)
-        y_copy(7, (1,), False)
+        y_quant(6, 1)
         y_quant(7, 0)
+        y_copy(7, (1,), False)
         y_quant(7, 1)
-        scales_out()

import math
from contextlib import ExitStack

import concourse.mybir as mybir
from concourse.masks import make_identity

B, NP, NC, T, N = 1024, 512, 1024, 1024, 1024
FLOPS = 2 * B * T * (NP + NC) + 2 * B * T * N

F32 = mybir.dt.float32
BF16 = mybir.dt.bfloat16
I32 = mybir.dt.int32
U32 = mybir.dt.uint32
U8 = mybir.dt.uint8
FP8X4 = mybir.dt.float8_e4m3fn_x4
FP4X4 = mybir.dt.float4_e2m1fn_x4
ALU = mybir.AluOpType
ACT = mybir.ActivationFunctionType

P = 128
G = 512
TILES = B // P
NUDGE = 1.5e-7
SCALE_STORES = [(0, 6), (6, 8)]
WORD_STORES = [(0, 2), (2, 4), (4, 6), (6, 7), (7, 8)]


def tile_partials_residual_features_k6_kernel(
    tc, freq, time, phase, partial_gain, amps, codes, atom_words, atom_scales,
    sample_gain, proj, note_gain, bias, feature_gain, out_0, out_1, out_2,
):
    nc = tc.nc
    with ExitStack() as ctx:
        keep = ctx.enter_context(tc.tile_pool(name="keep", bufs=1))
        work = ctx.enter_context(tc.tile_pool(name="work", bufs=2))
        psum = ctx.enter_context(tc.psum_pool(name="psum", bufs=1))
        ctx.enter_context(tc.manual_schedule())

        def kept(name, shape, dtype):
            return keep.tile(shape, dtype, name=name, align_bytes=64)

        def staged(name, shape, dtype, bufs):
            return work.tile(shape, dtype, name=name, tag=name, bufs=bufs, align_bytes=64)

        def bank_tile(n, shape, dtype):
            return psum.tile(shape, dtype, name="bank%d" % n, tag="bank%d" % n)

        warm = kept("warm", [P, 1], F32)
        warm_out = kept("warm_out", [P, 1], F32)
        ident32 = kept("ident32", [P, P], F32)
        ident16 = kept("ident16", [P, P], BF16)
        rows = kept("rows", [P, P], BF16)
        cols = kept("cols", [P, 16], F32)
        cols16 = kept("cols16", [P, 16], BF16)
        freq_sb = kept("freq_sb", [P, 4], BF16)
        phase_sb = kept("phase_sb", [P, 4], BF16)
        gain_sb = kept("gain_sb", [P, 4], BF16)
        freq_turns = kept("freq_turns", [P, 4], F32)
        phase_turns = kept("phase_turns", [P, 4], F32)
        two_pi = kept("two_pi", [P, 1], F32)
        time_sb = kept("time_sb", [P, 2, 4], BF16)
        bias_all = kept("bias_all", [P, N], BF16)
        fgain_all = kept("fgain_all", [P, N], F32)
        atom_raw = kept("atom_raw", [P, 2, 2 * T], U8)
        atom_codes = kept("atom_codes", [P, 2, 2 * T], U8)
        atom_sc_raw = kept("atom_sc_raw", [P, 2, T], U8)
        atom_sc = kept("atom_sc", [P, 2, T], U8)
        proj_raw = [kept("proj_raw%d" % h, [P, 4, N], BF16) for h in range(2)]
        proj_codes = kept("proj_codes", [P, 2, N], U32)
        proj_sc = kept("proj_sc", [P, 2, N], U8)
        bank_codes = kept("bank_codes", [P, T], U32)
        bank_sc = kept("bank_sc", [P, T], U8)
        x_codes = kept("x_codes", [P, 3 * TILES * P], U32)
        x_sc = kept("x_sc", [P, 3 * TILES * P], U8)
        y_codes = [kept("y_codes%d" % n, [P, 2, P * (b - a)], U32) for n, (a, b) in enumerate(WORD_STORES)]
        y_sc = [kept("y_sc%d" % n, [P, 2, P * (b - a)], U8) for n, (a, b) in enumerate(SCALE_STORES)]
        amps_raw = [kept("amps_raw%d" % j, [P, 2, NP], BF16) for j in range(TILES // 2)]
        codes_raw = [kept("codes_raw%d" % j, [P, 2, NC], BF16) for j in range(TILES // 2)]
        sines = [kept("sines%d" % h, [P, 4, G], F32) for h in range(2)]

        make_identity(nc, ident16[:])
        nc.vector.memset(atom_sc_raw[:].bitcast(I32), 0)
        nc.vector.memset(rows[:], 0.0)
        make_identity(nc, ident32[:])
        nc.vector.memset(warm[:], 1.0)
        nc.scalar.activation(out=warm_out[:], in_=warm[:], func=ACT.Silu)

        def load_x(j):
            rs = slice(2 * P * j, 2 * P * (j + 1))
            nc.sync.dma_start(out=amps_raw[j][:], in_=amps[rs, :].rearrange("(i p) k -> p i k", p=P))
            nc.sync.dma_start(out=codes_raw[j][:], in_=codes[rs, :].rearrange("(i p) k -> p i k", p=P))

        def load_proj(h):
            by_c = proj[G * h : G * (h + 1), :].rearrange("(a t c) f -> c a t f", t=4, c=4)
            for c in range(4):
                nc.sync.dma_start(out=proj_raw[h][c:P:4, :, :], in_=by_c[c])

        nc.sync.dma_start(out=time_sb[:], in_=time.rearrange("(h p r) -> p h r", h=2, r=4))
        nc.sync.dma_start(out=freq_sb[:], in_=freq.rearrange("(p s) -> p s", s=4))
        nc.sync.dma_start(out=phase_sb[:], in_=phase.rearrange("(p s) -> p s", s=4))
        load_x(0)
        nc.sync.dma_start(out=atom_raw[:].bitcast(I32), in_=atom_words.rearrange("g p n -> p g n").bitcast(I32))
        nc.sync.dma_start(out=gain_sb[:], in_=partial_gain.rearrange("(p s) -> p s", s=4))
        for q in range(4):
            nc.sync.dma_start(
                out=atom_sc_raw[32 * q : 32 * q + 4, :, :].bitcast(I32),
                in_=atom_scales[:, 4 * q : 4 * q + 4, :].rearrange("g r n -> r g n").bitcast(I32),
            )
        load_x(1)
        load_x(2)
        for h in range(2):
            nc.sync.dma_start(
                out=rows[4 * h : 4 * h + 4, :].rearrange("t (a c) -> t a c", c=4),
                in_=sample_gain[G * h : G * (h + 1)].rearrange("(a t c) -> t a c", t=4, c=4),
            )
        for n, vec in enumerate((note_gain, bias, feature_gain)):
            nc.sync.dma_start(out=rows[8 * n + 8 : 8 * n + 16, :], in_=vec.rearrange("(i p) -> i p", p=P))
        load_x(3)
        load_proj(0)
        load_proj(1)

        st = {}

        def x_at(i, q):
            return 6 * P * (i // 2) + 2 * P * q + P * (i % 2)

        def x_turn(n, bank):
            ps = bank_tile(bank, [P, 2, 2, P], F32)
            j, q = divmod(n, 3)
            for e in range(2):
                if q == 0:
                    words = amps_raw[j][:, e, :].bitcast(F32)
                else:
                    words = codes_raw[j][:, e, G * (q - 1) : G * q].bitcast(F32)
                for u in range(2):
                    nc.tensor.transpose(ps[:, e, u, :], words[:, u:256:2], ident32[:])
            st["xt", n] = ps

        def x_copy(n, on_vector):
            j, q = divmod(n, 3)
            if q == 0:
                st["xg", j, 0] = staged("amps_grouped", [P, 1, 8 * P], BF16, 2)
            elif ("xg", j, 1) not in st:
                st["xg", j, 1] = staged("codes_grouped", [P, 2, 8 * P], BF16, 2)
            copy = nc.vector.tensor_copy if on_vector else nc.scalar.copy
            copy(
                out=st["xg", j, min(q, 1)][:, max(q - 1, 0), :].bitcast(F32).rearrange("p (e b u) -> p e b u", e=2, u=2),
                in_=st["xt", n][:].rearrange("p e u b -> p e b u"),
            )

        def x_quant(j, part):
            at = x_at(2 * j, part)
            cs = slice(at, at + 2 * P * (part + 1))
            nc.vector.quantize_mx(
                out=x_codes[:, cs].bitcast(FP8X4), scales=x_sc[:, cs], in_=st["xg", j, part][:].rearrange("p q n -> p (q n)")
            )

        def spread_time(h, bank):
            st["time", h] = bank_tile(bank, [P, 4, P], BF16)
            for r in range(4):
                nc.tensor.transpose(st["time", h][:, r, :], time_sb[:, h, r : r + 1].to_broadcast([P, P]), ident16[:])

        def spread_row(n, bank):
            st["row", n] = bank_tile(bank, [P, 8, P], BF16)
            for r in range(8):
                col = cols16[:, 8 * n + r : 8 * n + r + 1]
                nc.tensor.transpose(st["row", n][:, r, :], col.to_broadcast([P, P]), ident16[:])

        def row_copy(n, on_vector):
            copy = nc.vector.tensor_copy if on_vector else nc.scalar.copy
            copy(out=(bias_all, fgain_all)[n][:], in_=st["row", n][:].rearrange("p r m -> p (r m)"))

        def rows_turn(bank):
            st["rows"] = bank_tile(bank, [P, P], BF16)
            nc.tensor.transpose(st["rows"][:], rows[:], ident16[:])

        def rows_copy():
            nc.scalar.copy(out=cols[:], in_=st["rows"][:, :16])
            nc.scalar.copy(out=cols16[:], in_=st["rows"][:, 16:32])

        def angle(h, s, on_vector):
            if ("u", h, s // 2) not in st:
                st["u", h, s // 2] = staged("turns", [P, 2, G], F32, 3)
            dst = st["u", h, s // 2][:, s % 2, :].rearrange("p (t a c) -> p t a c", t=4, c=4)
            src = st["time", h][:].rearrange("p c (a t) -> p t a c", t=4)
            f, ph = freq_turns[:, s : s + 1], phase_turns[:, s : s + 1]
            if on_vector:
                nc.vector.tensor_scalar(out=dst, in0=src, scalar1=f, scalar2=ph, op0=ALU.mult, op1=ALU.add)
            else:
                nc.scalar.activation(out=dst, in_=src, func=ACT.Identity, scale=f, bias=ph)

        def turns(h, s):
            k = staged("whole_turns", [P, 2, G], I32, 2)
            nc.vector.tensor_copy(out=k[:], in_=st["u", h, s][:])
            st["k", h, s] = k

        def frac(h, s):
            x = staged("frac", [P, 2, G], F32, 3)
            nc.vector.tensor_tensor(out=x[:], in0=st["u", h, s][:], in1=st["k", h, s][:], op=ALU.subtract)
            st["x", h, s] = x

        def sine(h, s):
            nc.scalar.activation(
                out=sines[h][:, 2 * s : 2 * s + 2, :], in_=st["x", h, s][:],
                func=ACT.Sin, scale=two_pi[:],
            )

        def bank_gain(h):
            grouped = staged("bank_grouped", [P, G, 4], BF16, 2)
            nc.vector.tensor_tensor(
                out=grouped[:].rearrange("p (j e) s -> p j s e", e=2),
                in0=sines[h][:].rearrange("p s (j e) -> p j s e", e=2),
                in1=gain_sb[:].unsqueeze(1).unsqueeze(3).to_broadcast([P, G // 2, 4, 2]),
                op=ALU.mult,
            )
            st["bg", h] = grouped

        def bank_quant(h):
            cs = slice(G * h, G * (h + 1))
            nc.vector.quantize_mx(
                out=bank_codes[:, cs].bitcast(FP8X4), scales=bank_sc[:, cs],
                in_=st["bg", h][:].rearrange("p j s -> p (j s)"),
            )

        def atom_order(h):
            ws = slice(256 * h, 256 * (h + 1))
            nc.vector.tensor_copy(
                out=atom_codes[:].bitcast(I32)[:, :, ws].rearrange("p g (t a c) -> p g t a c", t=4, c=2),
                in_=atom_raw[:].bitcast(I32)[:, :, ws].rearrange("p g (a t c) -> p g t a c", t=4, c=2),
            )

        def atom_scale_order():
            nc.vector.tensor_copy(
                out=atom_sc[:].bitcast(I32).rearrange("p g (h t a) -> p (g h) t a", h=2, t=4),
                in_=atom_sc_raw[:].bitcast(I32).rearrange("p g (h a t) -> p (g h) t a", h=2, t=4),
            )

        def proj_group(h, g, on_vector=False):
            grouped = staged("proj_grouped", [P, G, 4], BF16, 3)
            copy = nc.vector.tensor_copy if on_vector else nc.scalar.copy
            copy(
                out=grouped[:].rearrange("p (c i) t -> p c t i", i=4),
                in_=proj_raw[h][:, :, G * g : G * (g + 1)].rearrange("p t (c i) -> p c t i", i=4),
            )
            st["pg", h, g] = grouped

        def proj_quant(h, g):
            cs = slice(G * g, G * (g + 1))
            nc.vector.quantize_mx(
                out=proj_codes[:, h, cs].bitcast(FP8X4), scales=proj_sc[:, h, cs],
                in_=st["pg", h, g][:].rearrange("p c t -> p (c t)"),
            )

        def stage1(i, h, bank):
            ps = bank_tile(bank, [P, 4, P], F32)
            for t in range(4):
                c0 = G * h + P * t
                for g in range(2):
                    xs = slice(x_at(i, 1 + g), x_at(i, 1 + g) + P)
                    nc.tensor.matmul_mx(
                        out=ps[:, t, :], lhsT=atom_codes[:, g, 2 * c0 : 2 * (c0 + P)].bitcast(FP4X4),
                        lhsT_scale=atom_sc[:, g, c0 : c0 + P], rhs=x_codes[:, xs].bitcast(FP8X4),
                        rhs_scale=x_sc[:, xs], start=(g == 0), stop=False,
                    )
                xs = slice(x_at(i, 0), x_at(i, 0) + P)
                nc.tensor.matmul_mx(
                    out=ps[:, t, :], lhsT=bank_codes[:, c0 : c0 + P].bitcast(FP8X4),
                    lhsT_scale=bank_sc[:, c0 : c0 + P], rhs=x_codes[:, xs].bitcast(FP8X4),
                    rhs_scale=x_sc[:, xs], start=False, stop=True,
                )
            st["s1", i, h] = ps

        def wave(i, h):
            if ("wg", i) not in st:
                st["wg", i] = staged("wave_grouped", [P, 2, P, 4], BF16, 3)
            nc.vector.tensor_tensor(
                out=st["wg", i][:, h, :, :], in0=st["s1", i, h][:].rearrange("p t b -> p b t"),
                in1=cols[:, 4 * h : 4 * h + 4].unsqueeze(1).to_broadcast([P, P, 4]), op=ALU.mult,
            )

        def wave_quant(i):
            wc = staged("wave_codes", [P, 2 * P], U32, 4)
            ws = staged("wave_sc", [P, 2 * P], U8, 4)
            nc.vector.quantize_mx(
                out=wc[:].bitcast(FP8X4), scales=ws[:], in_=st["wg", i][:].rearrange("p h b t -> p (h b t)")
            )
            for h in range(2):
                st["wq", i, h] = (wc[:, P * h : P * (h + 1)], ws[:, P * h : P * (h + 1)])

        def stage2(i, g, bank):
            ps = bank_tile(bank, [P, G], F32)
            cs = slice(G * g, G * (g + 1))
            for h in range(2):
                wc, ws = st["wq", i, h]
                nc.tensor.matmul_mx(
                    out=ps[:], lhsT=wc.bitcast(FP8X4), lhsT_scale=ws,
                    rhs=proj_codes[:, h, cs].bitcast(FP8X4), rhs_scale=proj_sc[:, h, cs],
                    start=(h == 0), stop=(h == 1),
                )
            st["s2", i, g] = ps

        def affine(i, g):
            z = staged("pre_tanh", [P, G], F32, 4)
            nc.vector.scalar_tensor_tensor(
                out=z[:], in0=st["s2", i, g][:], scalar=cols[:, 8 + i : 9 + i],
                in1=bias_all[:, G * g : G * (g + 1)], op0=ALU.mult, op1=ALU.add,
            )
            st["z", i, g] = z

        def limiter(i, g):
            th = staged("limited", [P, G], F32, 4)
            nc.scalar.activation(out=th[:], in_=st["z", i, g][:], func=ACT.Tanh)
            st["th", i, g] = th

        def gain_out(i, g, on_pool):
            y = staged("y", [P, G], F32, 5)
            eng = nc.gpsimd if on_pool else nc.vector
            eng.tensor_tensor(out=y[:], in0=st["th", i, g][:], in1=fgain_all[:, G * g : G * (g + 1)], op=ALU.mult)
            st["y", i, g] = y
            nc.sync.dma_start(out=out_0[P * i : P * (i + 1), G * g : G * (g + 1)], in_=y[:])

        def y_round(i, g, on_vector):
            yb = staged("y_bf16", [P, G], BF16, 4)
            copy = nc.vector.tensor_copy if on_vector else nc.scalar.copy
            copy(
                out=yb[:].rearrange("p (u m e) -> p u m e", u=2, e=2),
                in_=st["y", i, g][:].rearrange("p (m u e) -> p u m e", u=2, e=2),
            )
            st["yb", i, g] = yb

        def y_turn(i, gs, bank):
            ps = bank_tile(bank, [P, len(gs), 2, P], F32)
            for n, g in enumerate(gs):
                words = st["yb", i, g][:].bitcast(F32)
                for u in range(2):
                    nc.tensor.transpose(ps[:, n, u, :], words[:, P * u : P * (u + 1)], ident32[:])
            st["yt", i, gs] = ps

        def y_copy(i, gs, on_vector):
            grouped = staged("y_grouped", [P, 2, P * 4], BF16, 3)
            copy = nc.vector.tensor_copy if on_vector else nc.scalar.copy
            copy(
                out=grouped[:, : len(gs), :].bitcast(F32).rearrange("p n (b u) -> p n b u", u=2),
                in_=st["yt", i, gs][:].rearrange("p n u b -> p n b u"),
            )
            for n, g in enumerate(gs):
                st["yg", i, g] = grouped[:, n, :]

        def y_quant(i, g):
            n = min(n for n, (a, b) in enumerate(WORD_STORES) if i < b)
            m = min(m for m, (a, b) in enumerate(SCALE_STORES) if i < b)
            at, sat = P * (i - WORD_STORES[n][0]), P * (i - SCALE_STORES[m][0])
            nc.vector.quantize_mx(
                out=y_codes[n][:, g, at : at + P].bitcast(FP8X4), scales=y_sc[m][:, g, sat : sat + P], in_=st["yg", i, g]
            )
            st["left", n] = st.get(("left", n), 2 * (WORD_STORES[n][1] - WORD_STORES[n][0])) - 1
            if st["left", n] == 0:
                ms = slice(P * WORD_STORES[n][0], P * WORD_STORES[n][1])
                nc.sync.dma_start(out=words_out[:, :, ms], in_=y_codes[n][:].bitcast(I32))
            st["sleft", m] = st.get(("sleft", m), 2 * (SCALE_STORES[m][1] - SCALE_STORES[m][0])) - 1
            if st["sleft", m] == 0:
                ms = slice(P * SCALE_STORES[m][0], P * SCALE_STORES[m][1])
                for q in range(4):
                    eng = nc.scalar if m == 1 and q % 2 == 0 else nc.sync
                    eng.dma_start(
                        out=out_2[:, 4 * q : 4 * q + 4, ms].rearrange("g r m -> r g m").bitcast(I32),
                        in_=y_sc[m][32 * q : 32 * q + 4, :, :].bitcast(I32),
                    )

        words_out = out_1.rearrange("g p m t -> p g (m t)").bitcast(I32)

        inv = 1.0 / (2.0 * math.pi)
        nc.vector.tensor_scalar(out=freq_turns[:], in0=freq_sb[:], scalar1=inv, scalar2=None, op0=ALU.mult)
        nc.vector.tensor_scalar(out=phase_turns[:], in0=phase_sb[:], scalar1=inv, scalar2=None, op0=ALU.mult)
        nc.vector.tensor_scalar(out=two_pi[:], in0=warm[:], scalar1=2.0 * math.pi - NUDGE, scalar2=NUDGE, op0=ALU.mult, op1=ALU.add)

        spread_time(0, 0)
        angle(0, 1, True)
        spread_time(1, 1)
        angle(0, 0, False)
        turns(0, 0)
        frac(0, 0)
        x_turn(2, 2)
        x_turn(0, 3)
        x_turn(1, 4)
        angle(0, 3, False)
        angle(0, 2, False)
        angle(1, 0, False)
        angle(1, 1, False)
        x_copy(2, False)
        angle(1, 3, False)
        x_copy(1, False)
        angle(1, 2, False)
        sine(0, 0)
        x_turn(3, 5)
        x_turn(4, 6)
        x_turn(5, 7)
        x_turn(8, 0)
        x_turn(6, 2)
        rows_turn(4)
        x_turn(7, 1)
        atom_order(0)
        turns(0, 1)
        turns(1, 0)
        frac(0, 1)
        frac(1, 0)
        atom_order(1)
        turns(1, 1)
        x_copy(0, False)
        x_quant(0, 0)
        x_quant(0, 1)
        frac(1, 1)
        sine(0, 1)
        sine(1, 0)
        x_copy(4, False)
        x_copy(3, False)
        x_copy(5, False)
        x_copy(6, False)
        bank_gain(0)
        x_quant(1, 1)
        x_quant(1, 0)
        bank_quant(0)
        atom_scale_order()
        rows_copy()
        spread_row(1, 3)
        spread_row(0, 6)
        x_turn(9, 5)
        x_turn(11, 7)
        x_turn(10, 2)
        sine(1, 1)
        x_copy(7, False)
        x_copy(8, False)
        row_copy(0, False)
        x_copy(9, False)
        x_copy(11, False)
        x_copy(10, False)
        proj_group(0, 1, False)
        proj_group(1, 1, False)
        bank_gain(1)
        x_quant(3, 0)
        stage1(2, 0, 4)
        stage1(0, 0, 1)
        bank_quant(1)
        wave(2, 0)
        x_quant(2, 1)
        x_quant(3, 1)
        stage1(0, 1, 0)
        wave(0, 1)
        wave(0, 0)
        x_quant(2, 0)
        stage1(2, 1, 6)
        stage1(1, 0, 5)
        stage1(1, 1, 7)
        proj_quant(0, 1)
        stage1(3, 1, 2)
        wave(2, 1)
        wave(1, 0)
        wave_quant(2)
        wave_quant(0)
        proj_quant(1, 1)
        proj_group(0, 0, False)
        proj_group(1, 0, False)
        wave(3, 1)
        wave(1, 1)
        stage1(3, 0, 4)
        stage2(0, 1, 0)
        wave(3, 0)
        affine(0, 1)
        wave_quant(3)
        wave_quant(1)
        proj_quant(0, 0)
        stage2(2, 1, 1)
        stage1(5, 1, 6)
        stage1(4, 1, 5)
        stage2(3, 1, 2)
        proj_quant(1, 0)
        affine(2, 1)
        row_copy(1, False)
        limiter(0, 1)
        stage2(1, 0, 7)
        stage2(0, 0, 4)
        stage1(5, 0, 0)
        stage2(3, 0, 1)
        stage1(4, 0, 3)
        gain_out(0, 1, True)
        limiter(2, 1)
        affine(3, 1)
        wave(4, 1)
        affine(1, 0)
        affine(0, 0)
        wave(5, 1)
        wave(5, 0)
        affine(3, 0)
        wave(4, 0)
        gain_out(2, 1, True)
        limiter(3, 1)
        y_round(0, 1, False)
        y_round(2, 1, False)
        limiter(0, 0)
        limiter(3, 0)
        limiter(1, 0)
        gain_out(3, 1, True)
        wave_quant(5)
        gain_out(0, 0, False)
        wave_quant(4)
        y_round(0, 0, False)
        y_round(3, 1, False)
        gain_out(1, 0, True)
        stage2(1, 1, 2)
        stage1(7, 1, 5)
        stage2(5, 1, 7)
        stage2(2, 0, 4)
        affine(1, 1)
        limiter(1, 1)
        gain_out(1, 1, True)
        stage2(4, 0, 6)
        y_turn(0, (0, 1), 0)
        stage2(4, 1, 1)
        stage2(5, 0, 3)
        stage1(7, 0, 2)
        affine(5, 1)
        affine(2, 0)
        gain_out(3, 0, False)
        y_round(1, 0, False)
        limiter(5, 1)
        y_copy(0, (0, 1), False)
        limiter(2, 0)
        gain_out(5, 1, True)
        wave(7, 1)
        affine(4, 0)
        affine(4, 1)
        affine(5, 0)
        wave(7, 0)
        y_round(1, 1, False)
        stage1(6, 0, 7)
        y_turn(1, (0, 1), 4)
        stage1(6, 1, 0)
        limiter(4, 1)
        limiter(5, 0)
        gain_out(2, 0, False)
        y_quant(0, 0)
        wave_quant(7)
        gain_out(4, 1, False)
        y_round(3, 0, False)
        y_round(2, 0, False)
        limiter(4, 0)
        y_copy(1, (0, 1), False)
        stage2(7, 0, 5)
        y_turn(2, (0, 1), 6)
        y_turn(3, (0, 1), 1)
        stage2(7, 1, 3)
        wave(6, 0)
        wave(6, 1)
        gain_out(5, 0, True)
        affine(7, 0)
        wave_quant(6)
        y_round(5, 1, True)
        y_quant(1, 1)
        y_quant(0, 1)
        gain_out(4, 0, False)
        y_quant(1, 0)
        stage2(6, 1, 2)
        stage2(6, 0, 4)
        affine(6, 1)
        affine(6, 0)
        affine(7, 1)
        y_round(4, 1, False)
        y_copy(2, (0, 1), False)
        limiter(7, 0)
        y_round(5, 0, False)
        y_round(4, 0, False)
        y_copy(3, (0, 1), False)
        limiter(6, 1)
        y_quant(3, 0)
        y_quant(2, 1)
        y_quant(2, 0)
        y_quant(3, 1)
        limiter(6, 0)
        gain_out(6, 1, False)
        y_turn(4, (0, 1), 7)
        y_turn(5, (0, 1), 0)
        y_copy(4, (0, 1), False)
        y_copy(5, (0, 1), False)
        limiter(7, 1)
        gain_out(6, 0, False)
        y_quant(4, 1)
        y_quant(4, 0)
        y_quant(5, 1)
        y_quant(5, 0)
        y_round(6, 1, True)
        y_round(6, 0, False)
        gain_out(7, 0, True)
        gain_out(7, 1, False)
        y_round(7, 1, True)
        y_round(7, 0, False)
        y_turn(6, (0, 1), 5)
        y_copy(6, (0, 1), False)
        y_turn(7, (0,), 2)
        y_turn(7, (1,), 4)
        y_copy(7, (0,), False)
        y_quant(6, 0)
        y_quant(6, 1)
        y_quant(7, 0)
        y_copy(7, (1,), False)
        y_quant(7, 1)
